import numpy as np
import ml_dtypes


def mxq(x, axis, fmt="e4m3"):
    dtype, down = {"e4m3": (ml_dtypes.float8_e4m3fn, 7), "e5m2": (ml_dtypes.float8_e5m2, 14)}[fmt]
    v = np.moveaxis(np.asarray(x, np.float32).astype(ml_dtypes.bfloat16).astype(np.float64), axis, -1)
    blocks = v.reshape(v.shape[:-1] + (-1, 32))
    amax = np.abs(blocks).max(-1, keepdims=True)
    byte = np.maximum(np.where(amax > 0, np.frexp(amax)[1] - 1 + 127, 0) - down, 1)
    scale = np.exp2(byte - 127.0)
    codes = (blocks / scale).astype(np.float32).astype(dtype).astype(np.float64)
    return np.moveaxis((codes * scale).reshape(v.shape), -1, axis)


WIDE = False


def mx_kscale(k):
    if not WIDE:
        return np.ones(k)
    levels = np.array([10, -10, 5, -5, 0])
    if k % 512:
        return np.exp2(np.random.permutation(np.resize(levels, k // 32))).repeat(32)
    a = np.empty((k // 512, 16))
    for p in range(k // 512):
        a[p, :8] = np.random.permutation(np.resize(levels, 8))
        for g in range(8):
            far = levels[np.abs(levels - a[p, g]) >= 10]
            a[p, g + 8] = far[np.random.randint(len(far))]
    return np.exp2(a.ravel()).repeat(32)


def f64(x):
    return np.asarray(x).astype(np.float64)


def striped(idx):
    return np.tile(idx.reshape(-1, 16).T, (8, 1)).astype(np.uint16)


def unstriped(offs):
    return offs[:16].T.reshape(-1).astype(np.int64)


E2M1 = np.array([0.0, 0.5, 1.0, 1.5, 2.0, 3.0, 4.0, 6.0, -0.0, -0.5, -1.0, -1.5, -2.0, -3.0, -4.0, -6.0])


def pack_weight(w, fmt):
    k, n = w.shape
    w = f64(np.asarray(w, np.float32).astype(ml_dtypes.bfloat16)).reshape(k // 32, 32, n)
    amax = np.abs(w).max(1)
    if fmt == "e4m3":
        byte = np.frexp(amax)[1] - 1 + 127 - 7
    else:
        mant, ex = np.frexp(amax / 6.0)
        byte = np.where(mant > 0.5, ex, ex - 1) + 127
    byte = np.clip(np.where(amax > 0, byte, 1), 1, 254)
    scaled = (w * np.exp2(127.0 - byte)[:, None, :]).reshape(k, n).astype(np.float32)
    by_word = np.ascontiguousarray(scaled.reshape(k // 512, 128, 4, n).transpose(0, 1, 3, 2))
    if fmt == "e4m3":
        words = by_word.astype(ml_dtypes.float8_e4m3fn).view(np.uint8)
    else:
        c = by_word.astype(ml_dtypes.float4_e2m1fn).view(np.uint8) & 0xF
        words = (c[..., 0::2] | (c[..., 1::2] << 4)).reshape(k // 512, 128, 2 * n)
    return np.ascontiguousarray(words), np.ascontiguousarray(byte.astype(np.uint8).reshape(k // 512, 16, n))


def unpack_weight(words, scales, fmt):
    g, _, n = scales.shape
    words = np.ascontiguousarray(words).reshape(g, 128, n, -1)
    if fmt == "e4m3":
        vals = words.view(ml_dtypes.float8_e4m3fn).astype(np.float64)
    else:
        nib = np.empty((g, 128, n, 4), np.uint8)
        nib[..., 0::2] = words & 0xF
        nib[..., 1::2] = words >> 4
        vals = E2M1[nib]
    vals = vals * np.repeat(np.exp2(scales.astype(np.float64) - 127.0), 8, axis=1)[..., None]
    return vals.transpose(0, 1, 3, 2).reshape(g * 512, n)


def gelu(v):
    return 0.5 * v * (1.0 + np.tanh(np.sqrt(2.0 / np.pi) * (v + 0.044715 * v**3)))


K, H, T, S, P, T3, S2 = 512, 1024, 4096, 1024, 512, 2048, 512

def setup_inputs():
    n = np.random.standard_normal
    s = mx_kscale(K)[:, None]
    u = mx_kscale(H)[:, None]
    tab_words, tab_scales = pack_weight(n((K, T)) * s, "e4m3")
    tab2_words, tab2_scales = pack_weight(n((H, T3)) / u / np.sqrt(H), "e4m3")
    w2_words, w2_scales = pack_weight(1.6 * n((K, H)) / s / np.sqrt(K), "e2m1")
    return {
        "tab_words": tab_words, "tab_scales": tab_scales,
        "offs": striped(np.random.permutation(T)[:S]),
        "tab2_words": tab2_words, "tab2_scales": tab2_scales,
        "offs2": striped(np.random.permutation(T3)[:S2]),
        "pos1": striped(np.random.permutation(S)[:P]),
        "pos2": striped(np.random.permutation(S)[:P]),
        "w1": (n((K, H)) / s / np.sqrt(K)).astype(np.float32),
        "w2_words": w2_words, "w2_scales": w2_scales,
        "pace": (0.8 * np.exp(0.3 * n(H))).astype(np.float32),
        "gain": (np.exp(0.3 * n(H)) * u[:, 0]).astype(np.float32),
        "down": (0.7 * n(H) * u[:, 0]).astype(np.float32),
        "base": (0.6 * n(S2)).astype(np.float32),
    }

def reference(tab_words, tab_scales, offs, tab2_words, tab2_scales, offs2, pos1, pos2,
              w1, w2_words, w2_scales, pace, gain, down, base):
    v = unpack_weight(tab_words, tab_scales, "e4m3")[:, unstriped(offs)]
    v2 = unpack_weight(tab2_words, tab2_scales, "e4m3")[:, unstriped(offs2)]
    w2 = unpack_weight(w2_words, w2_scales, "e2m1")
    y1 = mxq(f64(w1), 0, "e4m3").T @ v
    y2 = w2.T @ v
    h = f64(gain)[:, None] * (f64(pace)[:, None] * y1 + np.tanh(y2))
    x1 = mxq(h[:, unstriped(pos1)], 0, "e4m3")
    x2 = mxq(h[:, unstriped(pos2)] + f64(down)[:, None], 0, "e4m3")
    e1 = v2.T @ x1
    e2 = v2.T @ x2
    return e1 * e2 + f64(base)[:, None]

@@ -1,0 +1,250 @@
+from contextlib import ExitStack
+
+import concourse.mybir as mybir
+
+K, H, T, S, PJ, T3, S2 = 512, 1024, 4096, 1024, 512, 2048, 512
+FLOPS = 2 * (2 * K * H * S + 2 * H * S2 * PJ)
+
+F32 = mybir.dt.float32
+BF16 = mybir.dt.bfloat16
+I32 = mybir.dt.int32
+U32 = mybir.dt.uint32
+U16 = mybir.dt.uint16
+U8 = mybir.dt.uint8
+FP8X4 = mybir.dt.float8_e4m3fn_x4
+FP4X4 = mybir.dt.float4_e2m1fn_x4
+ACT = mybir.ActivationFunctionType
+ALU = mybir.AluOpType
+
+P = 128
+PACK = 4
+BANK = 512
+CHUNK = 256
+
+
+def tile_list_next_hut_advice_kernel(tc, tab_words, tab_scales, offs, tab2_words, tab2_scales, offs2, pos1, pos2,
+                                               w1, w2_words, w2_scales, pace, gain, down, base, out):
+    nc = tc.nc
+    with ExitStack() as ctx:
+        lists = ctx.enter_context(tc.tile_pool(name="lists", bufs=1))
+        keep = ctx.enter_context(tc.tile_pool(name="keep", bufs=1))
+        psum = ctx.enter_context(tc.psum_pool(name="psum", bufs=1))
+
+        def bank(n, shape, name):
+            return psum.tile(shape, F32, name=name, tag="bank%d" % n)
+
+        offs_t = lists.tile([P, S // 16], U16, name="offs_t")
+        offs2_t = lists.tile([P, S2 // 16], U16, name="offs2_t")
+        pos1_t = lists.tile([P, PJ // 16], U16, name="pos1_t")
+        pos2_t = lists.tile([P, PJ // 16], U16, name="pos2_t")
+
+        tab_s = keep.tile([P, T], U8, name="tab_s", align_bytes=64)
+        nc.vector.memset(tab_s[:].bitcast(I32), 0)
+        w2_s_raw = keep.tile([P, H], U8, name="w2_s_raw", align_bytes=64)
+        nc.vector.memset(w2_s_raw[:].bitcast(I32), 0)
+        tab2_s = keep.tile([P, T3], U8, name="tab2_s", align_bytes=64)
+        nc.vector.memset(tab2_s[:].bitcast(I32), 0)
+
+        def load_w1(b, half):
+            raw = keep.tile([P, PACK, 256], F32, name="w1_raw%d%d" % (b, half), tag="w1_raw%d" % half)
+            c0 = 512 * b + 256 * half
+            nc.sync.dma_start(raw[:], w1.rearrange("(p j) c -> p j c", j=PACK)[:, :, c0:c0 + 256])
+            return raw
+
+        def load_rows(vec, name):
+            vec_t = keep.tile([P, 2, PACK], F32, name=name)
+            nc.sync.dma_start(vec_t[:], vec.rearrange("(b p i) -> p b i", b=2, i=PACK))
+            return vec_t
+
+        nc.sync.dma_start(offs_t[:], offs)
+        nc.sync.dma_start(offs2_t[:], offs2)
+        nc.sync.dma_start(pos1_t[:], pos1)
+        nc.sync.dma_start(pos2_t[:], pos2)
+        pace_t = load_rows(pace, "pace_t")
+        w2_raw = keep.tile([P, 2 * H], U8, name="w2_raw", align_bytes=64)
+        nc.sync.dma_start(w2_raw[:].bitcast(I32), w2_words[0].bitcast(I32))
+        w1_raw = {(0, half): load_w1(0, half) for half in range(2)}
+        gain_t = load_rows(gain, "gain_t")
+        for q in range(4):
+            nc.sync.dma_start(tab_s[32 * q:32 * q + 4, :].bitcast(I32), tab_scales[0, 4 * q:4 * q + 4, :].bitcast(I32))
+        tab_w = keep.tile([P, T], I32, name="tab_w", tag="table_words", align_bytes=64)
+        nc.sync.dma_start(tab_w[:], tab_words[0].rearrange("p t i -> p (t i)").bitcast(I32))
+        for q in range(4):
+            nc.sync.dma_start(w2_s_raw[32 * q:32 * q + 4, :].bitcast(I32), w2_scales[0, 4 * q:4 * q + 4, :].bitcast(I32))
+        down_t = load_rows(down, "down_t")
+        for q in range(4):
+            nc.sync.dma_start(tab2_s[32 * q:32 * q + 8, :].bitcast(I32), tab2_scales[:, 4 * q:4 * q + 4, :].bitcast(I32))
+        base_t = keep.tile([P, 4], F32, name="base_t")
+        with nc.allow_non_contiguous_dma(reason="512 floats, one to a partition and hut tile"):
+            nc.sync.dma_start(base_t[:], base.rearrange("(t p) -> p t", p=P))
+
+        w2_c = keep.tile([P, 2 * H], U8, name="w2_c", align_bytes=64)
+        w2_s = keep.tile([P, H], U8, name="w2_s", align_bytes=64)
+        nc.vector.tensor_copy(w2_c[:].bitcast(U16).rearrange("p (b i m) -> p b i m", b=2, i=PACK),
+                              w2_raw[:].bitcast(U16).rearrange("p (b m i) -> p b i m", b=2, i=PACK))
+
+        v_s, v_w = [], []
+        for half in range(2):
+            vs = keep.tile([P, BANK], U8, name="v_s%d" % half, align_bytes=64)
+            nc.vector.tensor_copy(vs[:], tab_s[:].indirect(offs_t[:, 32 * half:32 * half + 32]))
+            v_s.append(vs)
+        for half in range(2):
+            vw = keep.tile([P, BANK], U32, name="v_w%d" % half, align_bytes=64)
+            nc.vector.tensor_copy(vw[:], tab_w[:].bitcast(U32).indirect(offs_t[:, 32 * half:32 * half + 32]))
+            v_w.append(vw)
+            if half == 0:
+                nc.vector.tensor_copy(w2_s[:].rearrange("p (b i m) -> p b i m", b=2, i=PACK),
+                                      w2_s_raw[:].rearrange("p (b m i) -> p b i m", b=2, i=PACK))
+
+        w1_c, w1_s = {}, {}
+
+        def round_w1(b, half, grouped):
+            dst = grouped[:, :, 64 * half:64 * half + 64, :].rearrange("p i m j -> p m i j")
+            nc.scalar.copy(dst, w1_raw[b, half][:].rearrange("p j (m i) -> p m i j", i=PACK))
+
+        def quantise_w1(b, grouped):
+            w1_c[b] = keep.tile([P, BANK], U32, name="w1_c%d" % b, align_bytes=64)
+            w1_s[b] = keep.tile([P, BANK], U8, name="w1_s%d" % b, align_bytes=64)
+            nc.vector.quantize_mx(out=w1_c[b][:].bitcast(FP8X4), scales=w1_s[b][:],
+                                  in_=grouped[:].rearrange("p i m j -> p (i m j)"))
+
+        grouped = [keep.tile([P, PACK, P, PACK], BF16, name="w1_grouped%d" % b, align_bytes=64) for b in range(2)]
+        for half in range(2):
+            round_w1(0, half, grouped[0])
+        quantise_w1(0, grouped[0])
+        for half in range(2):
+            w1_raw[1, half] = load_w1(1, half)
+        tab2_w = keep.tile([P, 2, T3], I32, name="tab2_w", tag="table_words", align_bytes=64)
+        nc.sync.dma_start(tab2_w[:], tab2_words.rearrange("a p t i -> p a (t i)").bitcast(I32))
+
+        th, hh = {}, {}
+
+        def tanh_tile(u):
+            th[u] = keep.tile([P, S], F32, name="th%d" % u)
+            for half in range(2):
+                y2 = bank((2 * u + half) % 4, [P, BANK], "y2")
+                nc.tensor.matmul_mx(out=y2[:], lhsT=w2_c[:, 256 * u:256 * u + 256].bitcast(FP4X4),
+                                    lhsT_scale=w2_s[:, P * u:P * u + P],
+                                    rhs=v_w[half][:].bitcast(FP8X4), rhs_scale=v_s[half][:], start=True, stop=True)
+                nc.scalar.activation(out=th[u][:, BANK * half:BANK * half + BANK], in_=y2[:], func=ACT.Tanh)
+
+        def join_tile(u):
+            b, i = divmod(u, PACK)
+            hh[u] = th[u]
+            for half in range(2):
+                y1 = bank(4 + (2 * u + half) % 4, [P, BANK], "y1")
+                nc.tensor.matmul_mx(out=y1[:], lhsT=w1_c[b][:, P * i:P * i + P].bitcast(FP8X4),
+                                    lhsT_scale=w1_s[b][:, P * i:P * i + P],
+                                    rhs=v_w[half][:].bitcast(FP8X4), rhs_scale=v_s[half][:], start=True, stop=True)
+                cols = slice(BANK * half, BANK * half + BANK)
+                nc.vector.scalar_tensor_tensor(out=hh[u][:, cols], in0=y1[:], scalar=pace_t[:, b, i:i + 1],
+                                               in1=th[u][:, cols], op0=ALU.mult, op1=ALU.add)
+
+        def pick_one(picked, pos_t, b, i, j0, width):
+            nc.vector.tensor_copy(picked[:, i, :], hh[PACK * b + i][:].indirect(pos_t[:, j0 // 16:(j0 + width) // 16]))
+
+        def pick(picked, pos_t, b, j0, width):
+            for i in range(PACK):
+                pick_one(picked, pos_t, b, i, j0, width)
+
+        def affine_one(planes, picked, with_down, b, i):
+            if with_down:
+                nc.scalar.activation(out=planes[:, i, :], in_=picked[:, i, :], func=ACT.Identity,
+                                     scale=gain_t[:, b, i:i + 1], bias=down_t[:, b, i:i + 1])
+            else:
+                nc.scalar.activation(out=planes[:, i, :], in_=picked[:, i, :], func=ACT.Copy, scale=gain_t[:, b, i:i + 1])
+
+        def affine(picked, with_down, b, width, name):
+            planes = keep.tile([P, PACK, width], BF16, name=name + "_planes", align_bytes=64)
+            for i in range(PACK):
+                affine_one(planes, picked, with_down, b, i)
+            return planes
+
+        def weave(planes, width, name, copy):
+            woven = keep.tile([P, width, PACK], BF16, name=name + "_woven", tag=name + "_woven", align_bytes=64)
+            copy(woven[:].rearrange("p (c n) i -> p c i n", n=4), planes[:].rearrange("p i (c n) -> p c i n", n=4))
+            return woven
+
+        def quantise_x(woven, width, name):
+            codes = keep.tile([P, width], U32, name=name + "_c", align_bytes=64)
+            scales = keep.tile([P, width], U8, name=name + "_s", align_bytes=64)
+            nc.vector.quantize_mx(out=codes[:].bitcast(FP8X4), scales=scales[:], in_=woven[:].rearrange("p n i -> p (n i)"))
+            return codes, scales
+
+        picked10 = keep.tile([P, PACK, PJ], F32, name="picked10")
+        picked11 = keep.tile([P, PACK, PJ], F32, name="picked11")
+        planes11 = keep.tile([P, PACK, PJ], BF16, name="x11_planes", align_bytes=64)
+        tanh_tile(0)
+        for u in range(4):
+            tanh_tile(u + 1)
+            if u < 2:
+                round_w1(1, u, grouped[1])
+            join_tile(u)
+            pick_one(picked10, pos1_t, 0, u, 0, PJ)
+            if u == 2:
+                quantise_w1(1, grouped[1])
+        planes10 = affine(picked10, False, 0, PJ, "x10")
+        for u in range(4, 8):
+            if u < 7:
+                tanh_tile(u + 1)
+            if u == 5:
+                woven10 = weave(planes10, PJ, "x10", nc.scalar.copy)
+            join_tile(u)
+            pick_one(picked11, pos1_t, 1, u - 4, 0, PJ)
+        for i in range(PACK):
+            affine_one(planes11, picked11, False, 1, i)
+        x10 = quantise_x(woven10, PJ, "x10")
+        woven11 = weave(planes11, PJ, "x11", nc.scalar.copy)
+
+        v2_s = keep.tile([P, S2], U8, name="v2_s", align_bytes=64)
+        nc.vector.tensor_copy(v2_s[:], tab2_s[:].indirect(offs2_t[:]))
+        v2_w = keep.tile([P, 2, S2], U32, name="v2_w", tag="x10_woven", align_bytes=64)
+        for a in range(2):
+            nc.vector.tensor_copy(v2_w[:, a, :], tab2_w[:, a, :].bitcast(U32).indirect(offs2_t[:]))
+        x11 = quantise_x(woven11, PJ, "x11")
+
+        def score(dst, a, mt, codes, scales, start, stop):
+            nc.tensor.matmul_mx(out=dst, lhsT=v2_w[:, a, P * mt:P * mt + P].bitcast(FP8X4),
+                                lhsT_scale=v2_s[4 * a:P, P * mt:P * mt + P],
+                                rhs=codes.bitcast(FP8X4), rhs_scale=scales, start=start, stop=stop)
+
+        e1_s = keep.tile([P, 4, PJ], F32, name="e1_s")
+        e1 = [bank(mt, [P, PJ], "e1") for mt in range(4)]
+        for mt in range(4):
+            score(e1[mt][:], 0, mt, x10[0][:], x10[1][:], True, False)
+        for mt in range(4):
+            score(e1[mt][:], 1, mt, x11[0][:], x11[1][:], False, True)
+            nc.scalar.copy(e1_s[:, mt, :], e1[mt][:])
+
+        picked2 = keep.tile([P, 2 * PACK * PJ], F32, name="picked2", tag="x11_woven", align_bytes=64)
+        picked20 = picked2[:, 0:PACK * PJ].rearrange("p (i n) -> p i n", i=PACK)
+        picked21 = picked2[:, PACK * PJ:].rearrange("p (c i n) -> p c i n", c=2, i=PACK)
+        pick(picked20, pos2_t, 0, 0, PJ)
+        for c in range(2):
+            pick(picked21[:, c], pos2_t, 1, CHUNK * c, CHUNK)
+        out_v = out.rearrange("(t p) j -> p t j", p=P)
+        x20 = quantise_x(weave(affine(picked20, True, 0, PJ, "x20"), PJ, "x20", nc.scalar.copy), PJ, "x20")
+        e2 = {}
+        for c in range(2):
+            cols = slice(CHUNK * c, CHUNK * c + CHUNK)
+            for q in range(2):
+                e2[c, q] = bank(4 + 2 * c + q, [P, 2, CHUNK], "e2")
+                for s in range(2):
+                    score(e2[c, q][:, s, :], 0, 2 * q + s, x20[0][:, cols], x20[1][:, cols], s == 0, False)
+        for c in range(2):
+            name = "x21%d" % c
+            planes = affine(picked21[:, c], True, 1, CHUNK, name)
+            woven = weave(planes, CHUNK, name, nc.vector.tensor_copy if c == 1 else nc.scalar.copy)
+            codes, scales = quantise_x(woven, CHUNK, name)
+            for q in range(2):
+                for s in range(2):
+                    score(e2[c, q][:, s, :], 1, 2 * q + s, codes[:], scales[:], False, s == 1)
+        for c in range(2):
+            cols = slice(CHUNK * c, CHUNK * c + CHUNK)
+            for q in range(2):
+                res = keep.tile([P, 2, CHUNK], F32, name="res%d%d" % (c, q))
+                nc.vector.tensor_tensor(res[:], e2[c, q][:], e1_s[:, 2 * q:2 * q + 2, cols], ALU.mult)
+                for s in range(2):
+                    mt = 2 * q + s
+                    nc.scalar.activation(out=res[:, s, :], in_=res[:, s, :], func=ACT.Identity, bias=base_t[:, mt:mt + 1])
+                nc.sync.dma_start(out_v[:, 2 * q:2 * q + 2, cols], res[:])

@@ -19,7 +19,8 @@ ALU = mybir.AluOpType
 P = 128
 PACK = 4
 BANK = 512
-CHUNK = 256
+CHUNKS = ((0, 256), (256, 128), (384, 128))
+OFF = (1, 2, 3, 4)
 
 
 def tile_list_next_hut_advice_kernel(tc, tab_words, tab_scales, offs, tab2_words, tab2_scales, offs2, pos1, pos2,
@@ -28,6 +29,7 @@ def tile_list_next_hut_advice_kernel(tc, tab_words, tab_scales, offs, tab2_words
     with ExitStack() as ctx:
         lists = ctx.enter_context(tc.tile_pool(name="lists", bufs=1))
         keep = ctx.enter_context(tc.tile_pool(name="keep", bufs=1))
+        ring = ctx.enter_context(tc.tile_pool(name="ring", bufs=4))
         psum = ctx.enter_context(tc.psum_pool(name="psum", bufs=1))
 
         def bank(n, shape, name):
@@ -71,12 +73,6 @@ def tile_list_next_hut_advice_kernel(tc, tab_words, tab_scales, offs, tab2_words
         nc.sync.dma_start(tab_w[:], tab_words[0].rearrange("p t i -> p (t i)").bitcast(I32))
         for q in range(4):
             nc.sync.dma_start(w2_s_raw[32 * q:32 * q + 4, :].bitcast(I32), w2_scales[0, 4 * q:4 * q + 4, :].bitcast(I32))
-        down_t = load_rows(down, "down_t")
-        for q in range(4):
-            nc.sync.dma_start(tab2_s[32 * q:32 * q + 8, :].bitcast(I32), tab2_scales[:, 4 * q:4 * q + 4, :].bitcast(I32))
-        base_t = keep.tile([P, 4], F32, name="base_t")
-        with nc.allow_non_contiguous_dma(reason="512 floats, one to a partition and hut tile"):
-            nc.sync.dma_start(base_t[:], base.rearrange("(t p) -> p t", p=P))
 
         w2_c = keep.tile([P, 2 * H], U8, name="w2_c", align_bytes=64)
         w2_s = keep.tile([P, H], U8, name="w2_s", align_bytes=64)
@@ -92,15 +88,14 @@ def tile_list_next_hut_advice_kernel(tc, tab_words, tab_scales, offs, tab2_words
             vw = keep.tile([P, BANK], U32, name="v_w%d" % half, align_bytes=64)
             nc.vector.tensor_copy(vw[:], tab_w[:].bitcast(U32).indirect(offs_t[:, 32 * half:32 * half + 32]))
             v_w.append(vw)
-            if half == 0:
-                nc.vector.tensor_copy(w2_s[:].rearrange("p (b i m) -> p b i m", b=2, i=PACK),
-                                      w2_s_raw[:].rearrange("p (b m i) -> p b i m", b=2, i=PACK))
+            nc.vector.tensor_copy(w2_s[:, 512 * half:512 * half + 512].rearrange("p (i m) -> p i m", i=PACK),
+                                  w2_s_raw[:, 512 * half:512 * half + 512].rearrange("p (m i) -> p i m", i=PACK))
 
         w1_c, w1_s = {}, {}
 
-        def round_w1(b, half, grouped):
+        def round_w1(b, half, grouped, copy):
             dst = grouped[:, :, 64 * half:64 * half + 64, :].rearrange("p i m j -> p m i j")
-            nc.scalar.copy(dst, w1_raw[b, half][:].rearrange("p j (m i) -> p m i j", i=PACK))
+            copy(dst, w1_raw[b, half][:].rearrange("p j (m i) -> p m i j", i=PACK))
 
         def quantise_w1(b, grouped):
             w1_c[b] = keep.tile([P, BANK], U32, name="w1_c%d" % b, align_bytes=64)
@@ -108,12 +103,23 @@ def tile_list_next_hut_advice_kernel(tc, tab_words, tab_scales, offs, tab2_words
             nc.vector.quantize_mx(out=w1_c[b][:].bitcast(FP8X4), scales=w1_s[b][:],
                                   in_=grouped[:].rearrange("p i m j -> p (i m j)"))
 
+        def gpsimd_round(dst, src):
+            nc.gpsimd.tensor_scalar(out=dst, in0=src, scalar1=1.0, scalar2=0.0, op0=ALU.mult, op1=ALU.add)
+
         grouped = [keep.tile([P, PACK, P, PACK], BF16, name="w1_grouped%d" % b, align_bytes=64) for b in range(2)]
         for half in range(2):
-            round_w1(0, half, grouped[0])
+            round_w1(0, half, grouped[0], nc.scalar.copy)
         quantise_w1(0, grouped[0])
         for half in range(2):
             w1_raw[1, half] = load_w1(1, half)
+            round_w1(1, half, grouped[1], gpsimd_round)
+        down_t = load_rows(down, "down_t")
+        for q in range(4):
+            nc.sync.dma_start(tab2_s[32 * q:32 * q + 8, :].bitcast(I32), tab2_scales[:, 4 * q:4 * q + 4, :].bitcast(I32))
+        base_t = keep.tile([P, 4], F32, name="base_t")
+        with nc.allow_non_contiguous_dma(reason="512 floats, one to a partition and hut tile"):
+            nc.sync.dma_start(base_t[:], base.rearrange("(t p) -> p t", p=P))
+
         tab2_w = keep.tile([P, 2, T3], I32, name="tab2_w", tag="table_words", align_bytes=64)
         nc.sync.dma_start(tab2_w[:], tab2_words.rearrange("a p t i -> p a (t i)").bitcast(I32))
 
@@ -137,8 +143,13 @@ def tile_list_next_hut_advice_kernel(tc, tab_words, tab_scales, offs, tab2_words
                                     lhsT_scale=w1_s[b][:, P * i:P * i + P],
                                     rhs=v_w[half][:].bitcast(FP8X4), rhs_scale=v_s[half][:], start=True, stop=True)
                 cols = slice(BANK * half, BANK * half + BANK)
-                nc.vector.scalar_tensor_tensor(out=hh[u][:, cols], in0=y1[:], scalar=pace_t[:, b, i:i + 1],
-                                               in1=th[u][:, cols], op0=ALU.mult, op1=ALU.add)
+                if u in OFF:
+                    paced = ring.tile([P, BANK], F32, name="paced", tag="paced")
+                    nc.scalar.activation(out=paced[:], in_=y1[:], func=ACT.Copy, scale=pace_t[:, b, i:i + 1])
+                    nc.gpsimd.tensor_tensor(hh[u][:, cols], paced[:], th[u][:, cols], ALU.add)
+                else:
+                    nc.vector.scalar_tensor_tensor(out=hh[u][:, cols], in0=y1[:], scalar=pace_t[:, b, i:i + 1],
+                                                   in1=th[u][:, cols], op0=ALU.mult, op1=ALU.add)
 
         def pick_one(picked, pos_t, b, i, j0, width):
             nc.vector.tensor_copy(picked[:, i, :], hh[PACK * b + i][:].indirect(pos_t[:, j0 // 16:(j0 + width) // 16]))
@@ -148,11 +159,8 @@ def tile_list_next_hut_advice_kernel(tc, tab_words, tab_scales, offs, tab2_words
                 pick_one(picked, pos_t, b, i, j0, width)
 
         def affine_one(planes, picked, with_down, b, i):
-            if with_down:
-                nc.scalar.activation(out=planes[:, i, :], in_=picked[:, i, :], func=ACT.Identity,
-                                     scale=gain_t[:, b, i:i + 1], bias=down_t[:, b, i:i + 1])
-            else:
-                nc.scalar.activation(out=planes[:, i, :], in_=picked[:, i, :], func=ACT.Copy, scale=gain_t[:, b, i:i + 1])
+            nc.gpsimd.tensor_scalar(out=planes[:, i, :], in0=picked[:, i, :], scalar1=gain_t[:, b, i:i + 1],
+                                    scalar2=down_t[:, b, i:i + 1] if with_down else 0.0, op0=ALU.mult, op1=ALU.add)
 
         def affine(picked, with_down, b, width, name):
             planes = keep.tile([P, PACK, width], BF16, name=name + "_planes", align_bytes=64)
@@ -172,39 +180,49 @@ def tile_list_next_hut_advice_kernel(tc, tab_words, tab_scales, offs, tab2_words
             return codes, scales
 
         picked10 = keep.tile([P, PACK, PJ], F32, name="picked10")
+        picked20 = keep.tile([P, PACK, PJ], F32, name="picked20")
         picked11 = keep.tile([P, PACK, PJ], F32, name="picked11")
+        planes10 = keep.tile([P, PACK, PJ], BF16, name="x10_planes", align_bytes=64)
+        planes20 = keep.tile([P, PACK, PJ], BF16, name="x20_planes", align_bytes=64)
         planes11 = keep.tile([P, PACK, PJ], BF16, name="x11_planes", align_bytes=64)
+        v2_s = keep.tile([P, S2], U8, name="v2_s", align_bytes=64)
         tanh_tile(0)
         for u in range(4):
             tanh_tile(u + 1)
-            if u < 2:
-                round_w1(1, u, grouped[1])
             join_tile(u)
             pick_one(picked10, pos1_t, 0, u, 0, PJ)
-            if u == 2:
+            if u == 1:
                 quantise_w1(1, grouped[1])
-        planes10 = affine(picked10, False, 0, PJ, "x10")
+            pick_one(picked20, pos2_t, 0, u, 0, PJ)
         for u in range(4, 8):
             if u < 7:
                 tanh_tile(u + 1)
+            join_tile(u)
+            if u == 4:
+                for i in range(PACK):
+                    affine_one(planes10, picked10, False, 0, i)
+                for i in range(PACK):
+                    affine_one(planes20, picked20, True, 0, i)
             if u == 5:
                 woven10 = weave(planes10, PJ, "x10", nc.scalar.copy)
-            join_tile(u)
+            if u == 6:
+                woven20 = weave(planes20, PJ, "x20", nc.scalar.copy)
             pick_one(picked11, pos1_t, 1, u - 4, 0, PJ)
-        for i in range(PACK):
-            affine_one(planes11, picked11, False, 1, i)
-        x10 = quantise_x(woven10, PJ, "x10")
+            affine_one(planes11, picked11, False, 1, u - 4)
+            if u == 6:
+                x10 = quantise_x(woven10, PJ, "x10")
+        x20 = quantise_x(woven20, PJ, "x20")
         woven11 = weave(planes11, PJ, "x11", nc.scalar.copy)
 
-        v2_s = keep.tile([P, S2], U8, name="v2_s", align_bytes=64)
         nc.vector.tensor_copy(v2_s[:], tab2_s[:].indirect(offs2_t[:]))
-        v2_w = keep.tile([P, 2, S2], U32, name="v2_w", tag="x10_woven", align_bytes=64)
+        v2_w = [keep.tile([P, S2], U32, name="v2_w0", align_bytes=64),
+                keep.tile([P, S2], U32, name="v2_w1", tag="x20_woven", align_bytes=64)]
         for a in range(2):
-            nc.vector.tensor_copy(v2_w[:, a, :], tab2_w[:, a, :].bitcast(U32).indirect(offs2_t[:]))
+            nc.vector.tensor_copy(v2_w[a][:], tab2_w[:, a, :].bitcast(U32).indirect(offs2_t[:]))
         x11 = quantise_x(woven11, PJ, "x11")
 
         def score(dst, a, mt, codes, scales, start, stop):
-            nc.tensor.matmul_mx(out=dst, lhsT=v2_w[:, a, P * mt:P * mt + P].bitcast(FP8X4),
+            nc.tensor.matmul_mx(out=dst, lhsT=v2_w[a][:, P * mt:P * mt + P].bitcast(FP8X4),
                                 lhsT_scale=v2_s[4 * a:P, P * mt:P * mt + P],
                                 rhs=codes.bitcast(FP8X4), rhs_scale=scales, start=start, stop=stop)
 
@@ -214,37 +232,41 @@ def tile_list_next_hut_advice_kernel(tc, tab_words, tab_scales, offs, tab2_words
             score(e1[mt][:], 0, mt, x10[0][:], x10[1][:], True, False)
         for mt in range(4):
             score(e1[mt][:], 1, mt, x11[0][:], x11[1][:], False, True)
-            nc.scalar.copy(e1_s[:, mt, :], e1[mt][:])
+        e2 = []
+        for c, (j0, width) in enumerate(CHUNKS):
+            per = BANK // width
+            for mt0 in range(0, 4, per):
+                acc = bank(4 + len(e2), [P, per, width], "e2")
+                e2.append((c, mt0, per, acc))
+                for s in range(per):
+                    score(acc[:, s, :], 0, mt0 + s, x20[0][:, j0:j0 + width], x20[1][:, j0:j0 + width], s == 0, False)
 
-        picked2 = keep.tile([P, 2 * PACK * PJ], F32, name="picked2", tag="x11_woven", align_bytes=64)
-        picked20 = picked2[:, 0:PACK * PJ].rearrange("p (i n) -> p i n", i=PACK)
-        picked21 = picked2[:, PACK * PJ:].rearrange("p (c i n) -> p c i n", c=2, i=PACK)
-        pick(picked20, pos2_t, 0, 0, PJ)
-        for c in range(2):
-            pick(picked21[:, c], pos2_t, 1, CHUNK * c, CHUNK)
+        picked21 = keep.tile([P, PACK * PJ], F32, name="picked21", tag="x11_woven", align_bytes=64)
+        planes21 = []
+        for c, (j0, width) in enumerate(CHUNKS):
+            picked = picked21[:, PACK * j0:PACK * (j0 + width)].rearrange("p (i n) -> p i n", i=PACK)
+            pick(picked, pos2_t, 1, j0, width)
+            planes21.append(affine(picked, True, 1, width, "x21%d" % c))
         out_v = out.rearrange("(t p) j -> p t j", p=P)
-        x20 = quantise_x(weave(affine(picked20, True, 0, PJ, "x20"), PJ, "x20", nc.scalar.copy), PJ, "x20")
-        e2 = {}
-        for c in range(2):
-            cols = slice(CHUNK * c, CHUNK * c + CHUNK)
-            for q in range(2):
-                e2[c, q] = bank(4 + 2 * c + q, [P, 2, CHUNK], "e2")
-                for s in range(2):
-                    score(e2[c, q][:, s, :], 0, 2 * q + s, x20[0][:, cols], x20[1][:, cols], s == 0, False)
-        for c in range(2):
+        for mt in range(2):
+            nc.scalar.copy(e1_s[:, mt, :], e1[mt][:])
+        woven21 = [weave(planes21[0], CHUNKS[0][1], "x210", nc.scalar.copy)]
+        for mt in range(2, 4):
+            nc.scalar.copy(e1_s[:, mt, :], e1[mt][:])
+        for c, (j0, width) in enumerate(CHUNKS):
             name = "x21%d" % c
-            planes = affine(picked21[:, c], True, 1, CHUNK, name)
-            woven = weave(planes, CHUNK, name, nc.vector.tensor_copy if c == 1 else nc.scalar.copy)
-            codes, scales = quantise_x(woven, CHUNK, name)
-            for q in range(2):
-                for s in range(2):
-                    score(e2[c, q][:, s, :], 1, 2 * q + s, codes[:], scales[:], False, s == 1)
-        for c in range(2):
-            cols = slice(CHUNK * c, CHUNK * c + CHUNK)
-            for q in range(2):
-                res = keep.tile([P, 2, CHUNK], F32, name="res%d%d" % (c, q))
-                nc.vector.tensor_tensor(res[:], e2[c, q][:], e1_s[:, 2 * q:2 * q + 2, cols], ALU.mult)
-                for s in range(2):
-                    mt = 2 * q + s
-                    nc.scalar.activation(out=res[:, s, :], in_=res[:, s, :], func=ACT.Identity, bias=base_t[:, mt:mt + 1])
-                nc.sync.dma_start(out_v[:, 2 * q:2 * q + 2, cols], res[:])
+            if c > 0:
+                woven21.append(weave(planes21[c], width, name, nc.scalar.copy if c == 1 else nc.vector.tensor_copy))
+            codes, scales = quantise_x(woven21[c], width, name)
+            for cc, mt0, per, acc in e2:
+                if cc == c:
+                    for s in range(per):
+                        score(acc[:, s, :], 1, mt0 + s, codes[:], scales[:], False, s == per - 1)
+        for c, mt0, per, acc in e2:
+            j0, width = CHUNKS[c]
+            res = keep.tile([P, per, width], F32, name="res%d%d" % (c, mt0))
+            nc.vector.tensor_tensor(res[:], acc[:], e1_s[:, mt0:mt0 + per, j0:j0 + width], ALU.mult)
+            for s in range(per):
+                mt = mt0 + s
+                nc.scalar.activation(out=res[:, s, :], in_=res[:, s, :], func=ACT.Identity, bias=base_t[:, mt:mt + 1])
+            nc.sync.dma_start(out_v[:, mt0:mt0 + per, j0:j0 + width], res[:])

@@ -21,6 +21,9 @@ PACK = 4
 BANK = 512
 CHUNKS = ((0, 256), (256, 128), (384, 128))
 OFF = (1, 2, 3, 4)
+AFF = "SGSGSS"
+CAST = "S"
+CAST_AT = 2
 
 
 def tile_list_next_hut_advice_kernel(tc, tab_words, tab_scales, offs, tab2_words, tab2_scales, offs2, pos1, pos2,
@@ -29,26 +32,29 @@ def tile_list_next_hut_advice_kernel(tc, tab_words, tab_scales, offs, tab2_words
     with ExitStack() as ctx:
         lists = ctx.enter_context(tc.tile_pool(name="lists", bufs=1))
         keep = ctx.enter_context(tc.tile_pool(name="keep", bufs=1))
-        ring = ctx.enter_context(tc.tile_pool(name="ring", bufs=4))
         psum = ctx.enter_context(tc.psum_pool(name="psum", bufs=1))
 
-        def bank(n, shape, name):
-            return psum.tile(shape, F32, name=name, tag="bank%d" % n)
+        taken = []
+
+        def bank(shape, name):
+            taken.append(name)
+            return psum.tile(shape, F32, name=name, tag="bank%d" % (len(taken) % 8))
 
         offs_t = lists.tile([P, S // 16], U16, name="offs_t")
         offs2_t = lists.tile([P, S2 // 16], U16, name="offs2_t")
         pos1_t = lists.tile([P, PJ // 16], U16, name="pos1_t")
         pos2_t = lists.tile([P, PJ // 16], U16, name="pos2_t")
 
-        tab_s = keep.tile([P, T], U8, name="tab_s", align_bytes=64)
-        nc.vector.memset(tab_s[:].bitcast(I32), 0)
-        w2_s_raw = keep.tile([P, H], U8, name="w2_s_raw", align_bytes=64)
+        w2_s_raw = keep.tile([P, H], U8, name="w2_s_raw", tag="w2_s_raw", align_bytes=64)
         nc.vector.memset(w2_s_raw[:].bitcast(I32), 0)
+        tab_s = keep.tile([P, T], U8, name="tab_s", tag="tab_s", align_bytes=64)
+        nc.vector.memset(tab_s[:].bitcast(I32), 0)
         tab2_s = keep.tile([P, T3], U8, name="tab2_s", align_bytes=64)
         nc.vector.memset(tab2_s[:].bitcast(I32), 0)
 
         def load_w1(b, half):
-            raw = keep.tile([P, PACK, 256], F32, name="w1_raw%d%d" % (b, half), tag="w1_raw%d" % half)
+            raw = keep.tile([P, PACK, 256], F32, name="w1_raw%d%d" % (b, half), align_bytes=64,
+                            tag={(0, 0): "th0", (0, 1): "w1_raw01", (1, 0): "w2_s_raw", (1, 1): "tab_s"}[b, half])
             c0 = 512 * b + 256 * half
             nc.sync.dma_start(raw[:], w1.rearrange("(p j) c -> p j c", j=PACK)[:, :, c0:c0 + 256])
             return raw
@@ -62,34 +68,34 @@ def tile_list_next_hut_advice_kernel(tc, tab_words, tab_scales, offs, tab2_words
         nc.sync.dma_start(offs2_t[:], offs2)
         nc.sync.dma_start(pos1_t[:], pos1)
         nc.sync.dma_start(pos2_t[:], pos2)
-        pace_t = load_rows(pace, "pace_t")
-        w2_raw = keep.tile([P, 2 * H], U8, name="w2_raw", align_bytes=64)
-        nc.sync.dma_start(w2_raw[:].bitcast(I32), w2_words[0].bitcast(I32))
-        w1_raw = {(0, half): load_w1(0, half) for half in range(2)}
-        gain_t = load_rows(gain, "gain_t")
-        for q in range(4):
-            nc.sync.dma_start(tab_s[32 * q:32 * q + 4, :].bitcast(I32), tab_scales[0, 4 * q:4 * q + 4, :].bitcast(I32))
-        tab_w = keep.tile([P, T], I32, name="tab_w", tag="table_words", align_bytes=64)
-        nc.sync.dma_start(tab_w[:], tab_words[0].rearrange("p t i -> p (t i)").bitcast(I32))
         for q in range(4):
             nc.sync.dma_start(w2_s_raw[32 * q:32 * q + 4, :].bitcast(I32), w2_scales[0, 4 * q:4 * q + 4, :].bitcast(I32))
+        for q in range(4):
+            nc.sync.dma_start(tab_s[32 * q:32 * q + 4, :].bitcast(I32), tab_scales[0, 4 * q:4 * q + 4, :].bitcast(I32))
+        w2_raw = keep.tile([P, 2 * H], U8, name="w2_raw", align_bytes=64)
+        nc.sync.dma_start(w2_raw[:].bitcast(I32), w2_words[0].bitcast(I32))
+        tab_w = keep.tile([P, T], I32, name="tab_w", tag="table_words", align_bytes=64)
+        nc.sync.dma_start(tab_w[:], tab_words[0].rearrange("p t i -> p (t i)").bitcast(I32))
+        w1_raw = {(0, half): load_w1(0, half) for half in range(2)}
+        pace_t = load_rows(pace, "pace_t")
+        gain_t = load_rows(gain, "gain_t")
 
         w2_c = keep.tile([P, 2 * H], U8, name="w2_c", align_bytes=64)
         w2_s = keep.tile([P, H], U8, name="w2_s", align_bytes=64)
-        nc.vector.tensor_copy(w2_c[:].bitcast(U16).rearrange("p (b i m) -> p b i m", b=2, i=PACK),
-                              w2_raw[:].bitcast(U16).rearrange("p (b m i) -> p b i m", b=2, i=PACK))
+        nc.vector.tensor_copy(w2_s[:].rearrange("p (b i m) -> p b i m", b=2, i=PACK),
+                              w2_s_raw[:].rearrange("p (b m i) -> p b i m", b=2, i=PACK))
 
         v_s, v_w = [], []
         for half in range(2):
             vs = keep.tile([P, BANK], U8, name="v_s%d" % half, align_bytes=64)
             nc.vector.tensor_copy(vs[:], tab_s[:].indirect(offs_t[:, 32 * half:32 * half + 32]))
             v_s.append(vs)
+        nc.vector.tensor_copy(w2_c[:].bitcast(U16).rearrange("p (b i m) -> p b i m", b=2, i=PACK),
+                              w2_raw[:].bitcast(U16).rearrange("p (b m i) -> p b i m", b=2, i=PACK))
         for half in range(2):
             vw = keep.tile([P, BANK], U32, name="v_w%d" % half, align_bytes=64)
             nc.vector.tensor_copy(vw[:], tab_w[:].bitcast(U32).indirect(offs_t[:, 32 * half:32 * half + 32]))
             v_w.append(vw)
-            nc.vector.tensor_copy(w2_s[:, 512 * half:512 * half + 512].rearrange("p (i m) -> p i m", i=PACK),
-                                  w2_s_raw[:, 512 * half:512 * half + 512].rearrange("p (m i) -> p i m", i=PACK))
 
         w1_c, w1_s = {}, {}
 
@@ -106,13 +112,14 @@ def tile_list_next_hut_advice_kernel(tc, tab_words, tab_scales, offs, tab2_words
         def gpsimd_round(dst, src):
             nc.gpsimd.tensor_scalar(out=dst, in0=src, scalar1=1.0, scalar2=0.0, op0=ALU.mult, op1=ALU.add)
 
-        grouped = [keep.tile([P, PACK, P, PACK], BF16, name="w1_grouped%d" % b, align_bytes=64) for b in range(2)]
-        for half in range(2):
-            round_w1(0, half, grouped[0], nc.scalar.copy)
+        grouped = [keep.tile([P, PACK, P, PACK], BF16, name="w1_grouped%d" % b, tag="w1_grouped%d" % b, align_bytes=64) for b in range(2)]
+        round_w1(0, 0, grouped[0], nc.scalar.copy)
+        round_w1(0, 1, grouped[0], nc.vector.tensor_copy)
         quantise_w1(0, grouped[0])
         for half in range(2):
             w1_raw[1, half] = load_w1(1, half)
-            round_w1(1, half, grouped[1], gpsimd_round)
+            if CAST == "G":
+                round_w1(1, half, grouped[1], gpsimd_round)
         down_t = load_rows(down, "down_t")
         for q in range(4):
             nc.sync.dma_start(tab2_s[32 * q:32 * q + 8, :].bitcast(I32), tab2_scales[:, 4 * q:4 * q + 4, :].bitcast(I32))
@@ -121,14 +128,15 @@ def tile_list_next_hut_advice_kernel(tc, tab_words, tab_scales, offs, tab2_words
             nc.sync.dma_start(base_t[:], base.rearrange("(t p) -> p t", p=P))
 
         tab2_w = keep.tile([P, 2, T3], I32, name="tab2_w", tag="table_words", align_bytes=64)
-        nc.sync.dma_start(tab2_w[:], tab2_words.rearrange("a p t i -> p a (t i)").bitcast(I32))
+        for a in range(2):
+            nc.sync.dma_start(tab2_w[:, a, :], tab2_words[a].rearrange("p t i -> p (t i)").bitcast(I32))
 
         th, hh = {}, {}
 
         def tanh_tile(u):
-            th[u] = keep.tile([P, S], F32, name="th%d" % u)
+            th[u] = keep.tile([P, S], F32, name="th%d" % u, tag="th%d" % u, align_bytes=64)
             for half in range(2):
-                y2 = bank((2 * u + half) % 4, [P, BANK], "y2")
+                y2 = bank([P, BANK], "y2")
                 nc.tensor.matmul_mx(out=y2[:], lhsT=w2_c[:, 256 * u:256 * u + 256].bitcast(FP4X4),
                                     lhsT_scale=w2_s[:, P * u:P * u + P],
                                     rhs=v_w[half][:].bitcast(FP8X4), rhs_scale=v_s[half][:], start=True, stop=True)
@@ -136,15 +144,15 @@ def tile_list_next_hut_advice_kernel(tc, tab_words, tab_scales, offs, tab2_words
 
         def join_tile(u):
             b, i = divmod(u, PACK)
-            hh[u] = th[u]
+            hh[u] = th[u] if u < 7 else keep.tile([P, S], F32, name="hh7", tag="x10_woven", align_bytes=64)
             for half in range(2):
-                y1 = bank(4 + (2 * u + half) % 4, [P, BANK], "y1")
+                y1 = bank([P, BANK], "y1")
                 nc.tensor.matmul_mx(out=y1[:], lhsT=w1_c[b][:, P * i:P * i + P].bitcast(FP8X4),
                                     lhsT_scale=w1_s[b][:, P * i:P * i + P],
                                     rhs=v_w[half][:].bitcast(FP8X4), rhs_scale=v_s[half][:], start=True, stop=True)
                 cols = slice(BANK * half, BANK * half + BANK)
                 if u in OFF:
-                    paced = ring.tile([P, BANK], F32, name="paced", tag="paced")
+                    paced = keep.tile([P, BANK], F32, name="paced", tag="paced%d%d" % (u, half), align_bytes=64)
                     nc.scalar.activation(out=paced[:], in_=y1[:], func=ACT.Copy, scale=pace_t[:, b, i:i + 1])
                     nc.gpsimd.tensor_tensor(hh[u][:, cols], paced[:], th[u][:, cols], ALU.add)
                 else:
@@ -158,23 +166,34 @@ def tile_list_next_hut_advice_kernel(tc, tab_words, tab_scales, offs, tab2_words
             for i in range(PACK):
                 pick_one(picked, pos_t, b, i, j0, width)
 
-        def affine_one(planes, picked, with_down, b, i):
-            nc.gpsimd.tensor_scalar(out=planes[:, i, :], in0=picked[:, i, :], scalar1=gain_t[:, b, i:i + 1],
-                                    scalar2=down_t[:, b, i:i + 1] if with_down else 0.0, op0=ALU.mult, op1=ALU.add)
+        def affine_one(planes, picked, with_down, b, i, eng):
+            if eng == "G":
+                nc.gpsimd.tensor_scalar(out=planes[:, i, :], in0=picked[:, i, :], scalar1=gain_t[:, b, i:i + 1],
+                                        scalar2=down_t[:, b, i:i + 1] if with_down else 0.0, op0=ALU.mult, op1=ALU.add)
+            elif with_down:
+                nc.scalar.activation(out=planes[:, i, :], in_=picked[:, i, :], func=ACT.Identity,
+                                     scale=gain_t[:, b, i:i + 1], bias=down_t[:, b, i:i + 1])
+            else:
+                nc.scalar.activation(out=planes[:, i, :], in_=picked[:, i, :], func=ACT.Copy, scale=gain_t[:, b, i:i + 1])
 
-        def affine(picked, with_down, b, width, name):
-            planes = keep.tile([P, PACK, width], BF16, name=name + "_planes", align_bytes=64)
+        def affine(picked, with_down, b, width, name, eng, tag):
+            planes = keep.tile([P, PACK, width], BF16, name=name + "_planes", tag=tag, align_bytes=64)
             for i in range(PACK):
-                affine_one(planes, picked, with_down, b, i)
+                affine_one(planes, picked, with_down, b, i, eng)
             return planes
 
-        def weave(planes, width, name, copy):
-            woven = keep.tile([P, width, PACK], BF16, name=name + "_woven", tag=name + "_woven", align_bytes=64)
+        def weave(planes, width, name, copy, tag=None):
+            woven = keep.tile([P, width, PACK], BF16, name=name + "_woven", tag=tag or name + "_woven", align_bytes=64)
             copy(woven[:].rearrange("p (c n) i -> p c i n", n=4), planes[:].rearrange("p i (c n) -> p c i n", n=4))
             return woven
 
-        def quantise_x(woven, width, name):
-            codes = keep.tile([P, width], U32, name=name + "_c", align_bytes=64)
+        def weave_gpsimd(planes, width, name):
+            woven = keep.tile([P, width, PACK], BF16, name=name + "_woven", tag=name + "_woven", align_bytes=64)
+            gpsimd_round(woven[:], planes[:].rearrange("p i n -> p n i"))
+            return woven
+
+        def quantise_x(woven, width, name, tag=None):
+            codes = keep.tile([P, width], U32, name=name + "_c", tag=tag or name + "_c", align_bytes=64)
             scales = keep.tile([P, width], U8, name=name + "_s", align_bytes=64)
             nc.vector.quantize_mx(out=codes[:].bitcast(FP8X4), scales=scales[:], in_=woven[:].rearrange("p n i -> p (n i)"))
             return codes, scales
@@ -182,43 +201,58 @@ def tile_list_next_hut_advice_kernel(tc, tab_words, tab_scales, offs, tab2_words
         picked10 = keep.tile([P, PACK, PJ], F32, name="picked10")
         picked20 = keep.tile([P, PACK, PJ], F32, name="picked20")
         picked11 = keep.tile([P, PACK, PJ], F32, name="picked11")
-        planes10 = keep.tile([P, PACK, PJ], BF16, name="x10_planes", align_bytes=64)
-        planes20 = keep.tile([P, PACK, PJ], BF16, name="x20_planes", align_bytes=64)
-        planes11 = keep.tile([P, PACK, PJ], BF16, name="x11_planes", align_bytes=64)
         v2_s = keep.tile([P, S2], U8, name="v2_s", align_bytes=64)
-        tanh_tile(0)
         for u in range(4):
-            tanh_tile(u + 1)
+            tanh_tile(u)
             join_tile(u)
-            pick_one(picked10, pos1_t, 0, u, 0, PJ)
-            if u == 1:
+            if u == 0:
+                nc.vector.tensor_copy(v2_s[:], tab2_s[:].indirect(offs2_t[:]))
+            if u == CAST_AT:
+                if CAST == "S":
+                    for half in range(2):
+                        round_w1(1, half, grouped[1], nc.scalar.copy)
                 quantise_w1(1, grouped[1])
+                v2_w.append(keep.tile([P, S2], U32, name="v2_w1", tag="w1_grouped1", align_bytes=64))
+                nc.vector.tensor_copy(v2_w[1][:], tab2_w[:, 1, :].bitcast(U32).indirect(offs2_t[:]))
+            pick_one(picked10, pos1_t, 0, u, 0, PJ)
             pick_one(picked20, pos2_t, 0, u, 0, PJ)
+            if u == 1:
+                v2_w = [keep.tile([P, S2], U32, name="v2_w0", align_bytes=64)]
+                nc.vector.tensor_copy(v2_w[0][:], tab2_w[:, 0, :].bitcast(U32).indirect(offs2_t[:]))
         for u in range(4, 8):
-            if u < 7:
-                tanh_tile(u + 1)
-            join_tile(u)
-            if u == 4:
-                for i in range(PACK):
-                    affine_one(planes10, picked10, False, 0, i)
-                for i in range(PACK):
-                    affine_one(planes20, picked20, True, 0, i)
-            if u == 5:
-                woven10 = weave(planes10, PJ, "x10", nc.scalar.copy)
-            if u == 6:
-                woven20 = weave(planes20, PJ, "x20", nc.scalar.copy)
-            pick_one(picked11, pos1_t, 1, u - 4, 0, PJ)
-            affine_one(planes11, picked11, False, 1, u - 4)
-            if u == 6:
+            tanh_tile(u)
+            if u in OFF:
+                join_tile(u)
+        last = max(OFF)
+        planes10 = keep.tile([P, PACK, PJ], BF16, name="x10_planes", tag="paced%d0" % last, align_bytes=64)
+        planes20 = keep.tile([P, PACK, PJ], BF16, name="x20_planes", tag="paced%d1" % last, align_bytes=64)
+        for i in range(PACK):
+            affine_one(planes10, picked10, False, 0, i, AFF[0])
+        for i in range(PACK):
+            affine_one(planes20, picked20, True, 0, i, AFF[1])
+        woven10 = weave(planes10, PJ, "x10", nc.scalar.copy)
+        woven20 = weave(planes20, PJ, "x20", nc.scalar.copy, "paced%d0" % last)
+        for u in range(4, 8):
+            if u == 7:
                 x10 = quantise_x(woven10, PJ, "x10")
-        x20 = quantise_x(woven20, PJ, "x20")
+            if u not in OFF:
+                join_tile(u)
+            pick_one(picked11, pos1_t, 1, u - 4, 0, PJ)
+        planes11 = keep.tile([P, PACK, PJ], BF16, name="x11_planes", tag="paced%d1" % last, align_bytes=64)
+        for i in range(PACK):
+            affine_one(planes11, picked11, False, 1, i, AFF[2])
         woven11 = weave(planes11, PJ, "x11", nc.scalar.copy)
 
-        nc.vector.tensor_copy(v2_s[:], tab2_s[:].indirect(offs2_t[:]))
-        v2_w = [keep.tile([P, S2], U32, name="v2_w0", align_bytes=64),
-                keep.tile([P, S2], U32, name="v2_w1", tag="x20_woven", align_bytes=64)]
-        for a in range(2):
-            nc.vector.tensor_copy(v2_w[a][:], tab2_w[:, a, :].bitcast(U32).indirect(offs2_t[:]))
+        planes21, woven21 = [], []
+
+        def pick21(c, tag):
+            j0, width = CHUNKS[c]
+            picked = keep.tile([P, PACK, width], F32, name="picked21%d" % c, tag=tag, align_bytes=64)
+            pick(picked, pos2_t, 1, j0, width)
+            planes21.append(affine(picked, True, 1, width, "x21%d" % c, AFF[3 + c], "planes21%d" % c))
+
+        x20 = quantise_x(woven20, PJ, "x20", "th7")
+        pick21(0, "paced%d0" % last)
         x11 = quantise_x(woven11, PJ, "x11")
 
         def score(dst, a, mt, codes, scales, start, stop):
@@ -227,7 +261,7 @@ def tile_list_next_hut_advice_kernel(tc, tab_words, tab_scales, offs, tab2_words
                                 rhs=codes.bitcast(FP8X4), rhs_scale=scales, start=start, stop=stop)
 
         e1_s = keep.tile([P, 4, PJ], F32, name="e1_s")
-        e1 = [bank(mt, [P, PJ], "e1") for mt in range(4)]
+        e1 = [bank([P, PJ], "e1") for mt in range(4)]
         for mt in range(4):
             score(e1[mt][:], 0, mt, x10[0][:], x10[1][:], True, False)
         for mt in range(4):
@@ -236,27 +270,21 @@ def tile_list_next_hut_advice_kernel(tc, tab_words, tab_scales, offs, tab2_words
         for c, (j0, width) in enumerate(CHUNKS):
             per = BANK // width
             for mt0 in range(0, 4, per):
-                acc = bank(4 + len(e2), [P, per, width], "e2")
+                acc = bank([P, per, width], "e2")
                 e2.append((c, mt0, per, acc))
                 for s in range(per):
                     score(acc[:, s, :], 0, mt0 + s, x20[0][:, j0:j0 + width], x20[1][:, j0:j0 + width], s == 0, False)
 
-        picked21 = keep.tile([P, PACK * PJ], F32, name="picked21", tag="x11_woven", align_bytes=64)
-        planes21 = []
-        for c, (j0, width) in enumerate(CHUNKS):
-            picked = picked21[:, PACK * j0:PACK * (j0 + width)].rearrange("p (i n) -> p i n", i=PACK)
-            pick(picked, pos2_t, 1, j0, width)
-            planes21.append(affine(picked, True, 1, width, "x21%d" % c))
+        woven21.append(weave(planes21[0], CHUNKS[0][1], "x210", nc.scalar.copy))
+        pick21(1, "x11_woven")
+        pick21(2, "planes210")
+        for mt in range(4):
+            nc.scalar.copy(e1_s[:, mt, :], e1[mt][:])
+        for c in range(1, len(CHUNKS)):
+            woven21.append(weave(planes21[c], CHUNKS[c][1], "x21%d" % c, nc.vector.tensor_copy))
         out_v = out.rearrange("(t p) j -> p t j", p=P)
-        for mt in range(2):
-            nc.scalar.copy(e1_s[:, mt, :], e1[mt][:])
-        woven21 = [weave(planes21[0], CHUNKS[0][1], "x210", nc.scalar.copy)]
-        for mt in range(2, 4):
-            nc.scalar.copy(e1_s[:, mt, :], e1[mt][:])
         for c, (j0, width) in enumerate(CHUNKS):
             name = "x21%d" % c
-            if c > 0:
-                woven21.append(weave(planes21[c], width, name, nc.scalar.copy if c == 1 else nc.vector.tensor_copy))
             codes, scales = quantise_x(woven21[c], width, name)
             for cc, mt0, per, acc in e2:
                 if cc == c:
@@ -264,7 +292,8 @@ def tile_list_next_hut_advice_kernel(tc, tab_words, tab_scales, offs, tab2_words
                         score(acc[:, s, :], 1, mt0 + s, codes[:], scales[:], False, s == per - 1)
         for c, mt0, per, acc in e2:
             j0, width = CHUNKS[c]
-            res = keep.tile([P, per, width], F32, name="res%d%d" % (c, mt0))
+            res = keep.tile([P, per, width], F32, name="res%d%d" % (c, mt0), align_bytes=64,
+                            tag="x212_woven" if (c, mt0) == (0, 0) else "res%d%d" % (c, mt0))
             nc.vector.tensor_tensor(res[:], acc[:], e1_s[:, mt0:mt0 + per, j0:j0 + width], ALU.mult)
             for s in range(per):
                 mt = mt0 + s

@@ -20,10 +20,11 @@ P = 128
 PACK = 4
 BANK = 512
 CHUNKS = ((0, 256), (256, 128), (384, 128))
-OFF = (1, 2, 3, 4)
-AFF = "SGSGSS"
-CAST = "S"
+OFF = (1, 2, 3, 4, 5)
+AFF = "SGSGGS"
+CAST = "GS"
 CAST_AT = 2
+SPLIT = 3
 
 
 def tile_list_next_hut_advice_kernel(tc, tab_words, tab_scales, offs, tab2_words, tab2_scales, offs2, pos1, pos2,
@@ -78,6 +79,8 @@ def tile_list_next_hut_advice_kernel(tc, tab_words, tab_scales, offs, tab2_words
         nc.sync.dma_start(tab_w[:], tab_words[0].rearrange("p t i -> p (t i)").bitcast(I32))
         w1_raw = {(0, half): load_w1(0, half) for half in range(2)}
         pace_t = load_rows(pace, "pace_t")
+        for q in range(4):
+            nc.sync.dma_start(tab2_s[32 * q:32 * q + 8, :].bitcast(I32), tab2_scales[:, 4 * q:4 * q + 4, :].bitcast(I32))
         gain_t = load_rows(gain, "gain_t")
 
         w2_c = keep.tile([P, 2 * H], U8, name="w2_c", align_bytes=64)
@@ -106,8 +109,9 @@ def tile_list_next_hut_advice_kernel(tc, tab_words, tab_scales, offs, tab2_words
         def quantise_w1(b, grouped):
             w1_c[b] = keep.tile([P, BANK], U32, name="w1_c%d" % b, align_bytes=64)
             w1_s[b] = keep.tile([P, BANK], U8, name="w1_s%d" % b, align_bytes=64)
-            nc.vector.quantize_mx(out=w1_c[b][:].bitcast(FP8X4), scales=w1_s[b][:],
-                                  in_=grouped[:].rearrange("p i m j -> p (i m j)"))
+            for i0, i1 in ((0, 1), (1, PACK)) if b == 0 else ((0, PACK),):
+                nc.vector.quantize_mx(out=w1_c[b][:, P * i0:P * i1].bitcast(FP8X4), scales=w1_s[b][:, P * i0:P * i1],
+                                      in_=grouped[:, i0:i1].rearrange("p i m j -> p (i m j)"))
 
         def gpsimd_round(dst, src):
             nc.gpsimd.tensor_scalar(out=dst, in0=src, scalar1=1.0, scalar2=0.0, op0=ALU.mult, op1=ALU.add)
@@ -118,11 +122,9 @@ def tile_list_next_hut_advice_kernel(tc, tab_words, tab_scales, offs, tab2_words
         quantise_w1(0, grouped[0])
         for half in range(2):
             w1_raw[1, half] = load_w1(1, half)
-            if CAST == "G":
+            if CAST[half] == "G":
                 round_w1(1, half, grouped[1], gpsimd_round)
         down_t = load_rows(down, "down_t")
-        for q in range(4):
-            nc.sync.dma_start(tab2_s[32 * q:32 * q + 8, :].bitcast(I32), tab2_scales[:, 4 * q:4 * q + 4, :].bitcast(I32))
         base_t = keep.tile([P, 4], F32, name="base_t")
         with nc.allow_non_contiguous_dma(reason="512 floats, one to a partition and hut tile"):
             nc.sync.dma_start(base_t[:], base.rearrange("(t p) -> p t", p=P))
@@ -201,15 +203,14 @@ def tile_list_next_hut_advice_kernel(tc, tab_words, tab_scales, offs, tab2_words
         picked10 = keep.tile([P, PACK, PJ], F32, name="picked10")
         picked20 = keep.tile([P, PACK, PJ], F32, name="picked20")
         picked11 = keep.tile([P, PACK, PJ], F32, name="picked11")
-        v2_s = keep.tile([P, S2], U8, name="v2_s", align_bytes=64)
+        v2_s = keep.tile([P, S2], U8, name="v2_s", tag="w1_grouped0", align_bytes=64)
+        nc.vector.tensor_copy(v2_s[:], tab2_s[:].indirect(offs2_t[:]))
         for u in range(4):
             tanh_tile(u)
             join_tile(u)
-            if u == 0:
-                nc.vector.tensor_copy(v2_s[:], tab2_s[:].indirect(offs2_t[:]))
             if u == CAST_AT:
-                if CAST == "S":
-                    for half in range(2):
+                for half in range(2):
+                    if CAST[half] == "S":
                         round_w1(1, half, grouped[1], nc.scalar.copy)
                 quantise_w1(1, grouped[1])
                 v2_w.append(keep.tile([P, S2], U32, name="v2_w1", tag="w1_grouped1", align_bytes=64))
@@ -277,7 +278,8 @@ def tile_list_next_hut_advice_kernel(tc, tab_words, tab_scales, offs, tab2_words
 
         woven21.append(weave(planes21[0], CHUNKS[0][1], "x210", nc.scalar.copy))
         pick21(1, "x11_woven")
-        pick21(2, "planes210")
+        if len(CHUNKS) > 2:
+            pick21(2, "planes210")
         for mt in range(4):
             nc.scalar.copy(e1_s[:, mt, :], e1[mt][:])
         for c in range(1, len(CHUNKS)):
@@ -290,12 +292,15 @@ def tile_list_next_hut_advice_kernel(tc, tab_words, tab_scales, offs, tab2_words
                 if cc == c:
                     for s in range(per):
                         score(acc[:, s, :], 1, mt0 + s, codes[:], scales[:], False, s == per - 1)
-        for c, mt0, per, acc in e2:
+        for c, bank_mt0, per, acc in e2:
             j0, width = CHUNKS[c]
-            res = keep.tile([P, per, width], F32, name="res%d%d" % (c, mt0), align_bytes=64,
-                            tag="x212_woven" if (c, mt0) == (0, 0) else "res%d%d" % (c, mt0))
-            nc.vector.tensor_tensor(res[:], acc[:], e1_s[:, mt0:mt0 + per, j0:j0 + width], ALU.mult)
-            for s in range(per):
-                mt = mt0 + s
-                nc.scalar.activation(out=res[:, s, :], in_=res[:, s, :], func=ACT.Identity, bias=base_t[:, mt:mt + 1])
-            nc.sync.dma_start(out_v[:, mt0:mt0 + per, j0:j0 + width], res[:])
+            step = 2 if c >= SPLIT else per
+            for s0 in range(0, per, step):
+                mt0 = bank_mt0 + s0
+                res = keep.tile([P, step, width], F32, name="res%d%d" % (c, mt0), align_bytes=64,
+                                tag="x21%d_woven" % (len(CHUNKS) - 1) if (c, mt0) == (0, 0) else "res%d%d" % (c, mt0))
+                nc.vector.tensor_tensor(res[:], acc[:, s0:s0 + step, :], e1_s[:, mt0:mt0 + step, j0:j0 + width], ALU.mult)
+                for s in range(step):
+                    mt = mt0 + s
+                    nc.scalar.activation(out=res[:, s, :], in_=res[:, s, :], func=ACT.Identity, bias=base_t[:, mt:mt + 1])
+                nc.sync.dma_start(out_v[:, mt0:mt0 + step, j0:j0 + width], res[:])

@@ -2,8 +2,8 @@ from contextlib import ExitStack
 
 import concourse.mybir as mybir
 
-K, H, T, S, PJ, T3, S2 = 512, 1024, 4096, 1024, 512, 2048, 512
-FLOPS = 2 * (2 * K * H * S + 2 * H * S2 * PJ)
+K, H, T, S, PAIRS, T2, HUTS = 512, 1024, 4096, 1024, 512, 2048, 512
+FLOPS = 2 * (2 * K * H * S + 2 * H * HUTS * PAIRS)
 
 F32 = mybir.dt.float32
 BF16 = mybir.dt.bfloat16
@@ -18,13 +18,16 @@ ALU = mybir.AluOpType
 
 P = 128
 PACK = 4
+PER_COLUMN = 16
 BANK = 512
-CHUNKS = ((0, 256), (256, 128), (384, 128))
-OFF = (1, 2, 3, 4, 5)
-AFF = "SGSGGS"
-CAST = "GS"
-CAST_AT = 2
-SPLIT = 3
+BANKS = 8
+ROW_TILES = H // P
+HUT_TILES = HUTS // P
+W1_PIECE = 256
+CHUNK = PAIRS // 2
+FIRST_SHARED, LAST_SHARED = 1, 5
+W1_SECOND_AFTER = 2
+E1_EARLY = 2
 
 
 def tile_list_next_hut_advice_kernel(tc, tab_words, tab_scales, offs, tab2_words, tab2_scales, offs2, pos1, pos2,
@@ -35,32 +38,31 @@ def tile_list_next_hut_advice_kernel(tc, tab_words, tab_scales, offs, tab2_words
         keep = ctx.enter_context(tc.tile_pool(name="keep", bufs=1))
         psum = ctx.enter_context(tc.psum_pool(name="psum", bufs=1))
 
-        taken = []
+        banks_taken = []
 
-        def bank(shape, name):
-            taken.append(name)
-            return psum.tile(shape, F32, name=name, tag="bank%d" % (len(taken) % 8))
+        def next_bank(shape, name):
+            banks_taken.append(name)
+            return psum.tile(shape, F32, name=name, tag="bank%d" % (len(banks_taken) % BANKS))
 
-        offs_t = lists.tile([P, S // 16], U16, name="offs_t")
-        offs2_t = lists.tile([P, S2 // 16], U16, name="offs2_t")
-        pos1_t = lists.tile([P, PJ // 16], U16, name="pos1_t")
-        pos2_t = lists.tile([P, PJ // 16], U16, name="pos2_t")
+        offs_t = lists.tile([P, S // PER_COLUMN], U16, name="offs_t")
+        offs2_t = lists.tile([P, HUTS // PER_COLUMN], U16, name="offs2_t")
+        pos1_t = lists.tile([P, PAIRS // PER_COLUMN], U16, name="pos1_t")
+        pos2_t = lists.tile([P, PAIRS // PER_COLUMN], U16, name="pos2_t")
 
-        w2_s_raw = keep.tile([P, H], U8, name="w2_s_raw", tag="w2_s_raw", align_bytes=64)
-        nc.vector.memset(w2_s_raw[:].bitcast(I32), 0)
-        tab_s = keep.tile([P, T], U8, name="tab_s", tag="tab_s", align_bytes=64)
-        nc.vector.memset(tab_s[:].bitcast(I32), 0)
-        tab2_s = keep.tile([P, T3], U8, name="tab2_s", align_bytes=64)
-        nc.vector.memset(tab2_s[:].bitcast(I32), 0)
+        w2_scales_raw = keep.tile([P, H], U8, name="w2_scales_raw", tag="w2_scales_raw", align_bytes=64)
+        nc.vector.memset(w2_scales_raw[:].bitcast(I32), 0)
+        tab_scale_t = keep.tile([P, T], U8, name="tab_scale_t", tag="tab_scale_t", align_bytes=64)
+        nc.vector.memset(tab_scale_t[:].bitcast(I32), 0)
+        tab2_scale_t = keep.tile([P, T2], U8, name="tab2_scale_t", align_bytes=64)
+        nc.vector.memset(tab2_scale_t[:].bitcast(I32), 0)
 
-        def load_w1(b, half):
-            raw = keep.tile([P, PACK, 256], F32, name="w1_raw%d%d" % (b, half), align_bytes=64,
-                            tag={(0, 0): "th0", (0, 1): "w1_raw01", (1, 0): "w2_s_raw", (1, 1): "tab_s"}[b, half])
-            c0 = 512 * b + 256 * half
-            nc.sync.dma_start(raw[:], w1.rearrange("(p j) c -> p j c", j=PACK)[:, :, c0:c0 + 256])
+        def load_w1(b, piece, tag):
+            raw = keep.tile([P, PACK, W1_PIECE], F32, name="w1_raw%d%d" % (b, piece), tag=tag, align_bytes=64)
+            c0 = BANK * b + W1_PIECE * piece
+            nc.sync.dma_start(raw[:], w1.rearrange("(p j) c -> p j c", j=PACK)[:, :, c0:c0 + W1_PIECE])
             return raw
 
-        def load_rows(vec, name):
+        def load_by_row(vec, name):
             vec_t = keep.tile([P, 2, PACK], F32, name=name)
             nc.sync.dma_start(vec_t[:], vec.rearrange("(b p i) -> p b i", b=2, i=PACK))
             return vec_t
@@ -70,237 +72,242 @@ def tile_list_next_hut_advice_kernel(tc, tab_words, tab_scales, offs, tab2_words
         nc.sync.dma_start(pos1_t[:], pos1)
         nc.sync.dma_start(pos2_t[:], pos2)
         for q in range(4):
-            nc.sync.dma_start(w2_s_raw[32 * q:32 * q + 4, :].bitcast(I32), w2_scales[0, 4 * q:4 * q + 4, :].bitcast(I32))
+            nc.sync.dma_start(w2_scales_raw[32 * q:32 * q + 4, :].bitcast(I32), w2_scales[0, 4 * q:4 * q + 4, :].bitcast(I32))
         for q in range(4):
-            nc.sync.dma_start(tab_s[32 * q:32 * q + 4, :].bitcast(I32), tab_scales[0, 4 * q:4 * q + 4, :].bitcast(I32))
-        w2_raw = keep.tile([P, 2 * H], U8, name="w2_raw", align_bytes=64)
-        nc.sync.dma_start(w2_raw[:].bitcast(I32), w2_words[0].bitcast(I32))
-        tab_w = keep.tile([P, T], I32, name="tab_w", tag="table_words", align_bytes=64)
-        nc.sync.dma_start(tab_w[:], tab_words[0].rearrange("p t i -> p (t i)").bitcast(I32))
-        w1_raw = {(0, half): load_w1(0, half) for half in range(2)}
-        pace_t = load_rows(pace, "pace_t")
+            nc.sync.dma_start(tab_scale_t[32 * q:32 * q + 4, :].bitcast(I32), tab_scales[0, 4 * q:4 * q + 4, :].bitcast(I32))
+        w2_words_raw = keep.tile([P, 2 * H], U8, name="w2_words_raw", align_bytes=64)
+        nc.sync.dma_start(w2_words_raw[:].bitcast(I32), w2_words[0].bitcast(I32))
+        tab_word_t = keep.tile([P, T], I32, name="tab_word_t", tag="table_words", align_bytes=64)
+        nc.sync.dma_start(tab_word_t[:], tab_words[0].rearrange("p t i -> p (t i)").bitcast(I32))
+        w1_raw = {(0, 0): load_w1(0, 0, "row_tile0"), (0, 1): load_w1(0, 1, "w1_raw01")}
+        pace_t = load_by_row(pace, "pace_t")
+        w1_raw[1, 0] = load_w1(1, 0, "w2_scales_raw")
         for q in range(4):
-            nc.sync.dma_start(tab2_s[32 * q:32 * q + 8, :].bitcast(I32), tab2_scales[:, 4 * q:4 * q + 4, :].bitcast(I32))
-        gain_t = load_rows(gain, "gain_t")
+            nc.sync.dma_start(tab2_scale_t[32 * q:32 * q + 8, :].bitcast(I32), tab2_scales[:, 4 * q:4 * q + 4, :].bitcast(I32))
+        gain_t = load_by_row(gain, "gain_t")
 
-        w2_c = keep.tile([P, 2 * H], U8, name="w2_c", align_bytes=64)
-        w2_s = keep.tile([P, H], U8, name="w2_s", align_bytes=64)
-        nc.vector.tensor_copy(w2_s[:].rearrange("p (b i m) -> p b i m", b=2, i=PACK),
-                              w2_s_raw[:].rearrange("p (b m i) -> p b i m", b=2, i=PACK))
+        w2_codes = keep.tile([P, 2 * H], U8, name="w2_codes", align_bytes=64)
+        w2_plane = keep.tile([P, H], U8, name="w2_plane", align_bytes=64)
+        nc.vector.tensor_copy(w2_plane[:].rearrange("p (b i m) -> p b i m", b=2, i=PACK),
+                              w2_scales_raw[:].rearrange("p (b m i) -> p b i m", b=2, i=PACK))
 
-        v_s, v_w = [], []
+        half_columns = BANK // PER_COLUMN
+        v_plane, v_codes = [], []
         for half in range(2):
-            vs = keep.tile([P, BANK], U8, name="v_s%d" % half, align_bytes=64)
-            nc.vector.tensor_copy(vs[:], tab_s[:].indirect(offs_t[:, 32 * half:32 * half + 32]))
-            v_s.append(vs)
-        nc.vector.tensor_copy(w2_c[:].bitcast(U16).rearrange("p (b i m) -> p b i m", b=2, i=PACK),
-                              w2_raw[:].bitcast(U16).rearrange("p (b m i) -> p b i m", b=2, i=PACK))
+            plane = keep.tile([P, BANK], U8, name="v_plane%d" % half, align_bytes=64)
+            nc.vector.tensor_copy(plane[:], tab_scale_t[:].indirect(offs_t[:, half_columns * half:half_columns * (half + 1)]))
+            v_plane.append(plane)
+        nc.vector.tensor_copy(w2_codes[:].bitcast(U16).rearrange("p (b i m) -> p b i m", b=2, i=PACK),
+                              w2_words_raw[:].bitcast(U16).rearrange("p (b m i) -> p b i m", b=2, i=PACK))
         for half in range(2):
-            vw = keep.tile([P, BANK], U32, name="v_w%d" % half, align_bytes=64)
-            nc.vector.tensor_copy(vw[:], tab_w[:].bitcast(U32).indirect(offs_t[:, 32 * half:32 * half + 32]))
-            v_w.append(vw)
+            codes = keep.tile([P, BANK], U32, name="v_codes%d" % half, align_bytes=64)
+            nc.vector.tensor_copy(codes[:], tab_word_t[:].bitcast(U32).indirect(offs_t[:, half_columns * half:half_columns * (half + 1)]))
+            v_codes.append(codes)
 
-        w1_c, w1_s = {}, {}
+        w1_codes, w1_plane = {}, {}
+        w1_bf16 = [keep.tile([P, PACK, P, PACK], BF16, name="w1_bf16_%d" % b, tag="w1_bf16_%d" % b, align_bytes=64) for b in range(2)]
 
-        def round_w1(b, half, grouped, copy):
-            dst = grouped[:, :, 64 * half:64 * half + 64, :].rearrange("p i m j -> p m i j")
-            copy(dst, w1_raw[b, half][:].rearrange("p j (m i) -> p m i j", i=PACK))
-
-        def quantise_w1(b, grouped):
-            w1_c[b] = keep.tile([P, BANK], U32, name="w1_c%d" % b, align_bytes=64)
-            w1_s[b] = keep.tile([P, BANK], U8, name="w1_s%d" % b, align_bytes=64)
-            for i0, i1 in ((0, 1), (1, PACK)) if b == 0 else ((0, PACK),):
-                nc.vector.quantize_mx(out=w1_c[b][:, P * i0:P * i1].bitcast(FP8X4), scales=w1_s[b][:, P * i0:P * i1],
-                                      in_=grouped[:, i0:i1].rearrange("p i m j -> p (i m j)"))
+        def round_w1(b, piece, copy):
+            m0, m1 = W1_PIECE // PACK * piece, W1_PIECE // PACK * (piece + 1)
+            copy(w1_bf16[b][:, :, m0:m1, :].rearrange("p i m j -> p m i j"),
+                 w1_raw[b, piece][:].rearrange("p j (m i) -> p m i j", i=PACK))
 
         def gpsimd_round(dst, src):
             nc.gpsimd.tensor_scalar(out=dst, in0=src, scalar1=1.0, scalar2=0.0, op0=ALU.mult, op1=ALU.add)
 
-        grouped = [keep.tile([P, PACK, P, PACK], BF16, name="w1_grouped%d" % b, tag="w1_grouped%d" % b, align_bytes=64) for b in range(2)]
-        round_w1(0, 0, grouped[0], nc.scalar.copy)
-        round_w1(0, 1, grouped[0], nc.vector.tensor_copy)
-        quantise_w1(0, grouped[0])
-        for half in range(2):
-            w1_raw[1, half] = load_w1(1, half)
-            if CAST[half] == "G":
-                round_w1(1, half, grouped[1], gpsimd_round)
-        down_t = load_rows(down, "down_t")
-        base_t = keep.tile([P, 4], F32, name="base_t")
-        with nc.allow_non_contiguous_dma(reason="512 floats, one to a partition and hut tile"):
+        def quantise_w1(b, cuts):
+            w1_codes[b] = keep.tile([P, BANK], U32, name="w1_codes%d" % b, align_bytes=64)
+            w1_plane[b] = keep.tile([P, BANK], U8, name="w1_plane%d" % b, align_bytes=64)
+            for i0, i1 in cuts:
+                nc.vector.quantize_mx(out=w1_codes[b][:, P * i0:P * i1].bitcast(FP8X4), scales=w1_plane[b][:, P * i0:P * i1],
+                                      in_=w1_bf16[b][:, i0:i1].rearrange("p i m j -> p (i m j)"))
+
+        round_w1(0, 0, nc.scalar.copy)
+        round_w1(0, 1, nc.vector.tensor_copy)
+        quantise_w1(0, ((0, 1), (1, PACK)))
+        round_w1(1, 0, gpsimd_round)
+        w1_raw[1, 1] = load_w1(1, 1, "tab_scale_t")
+        down_t = load_by_row(down, "down_t")
+        base_t = keep.tile([P, HUT_TILES], F32, name="base_t")
+        with nc.allow_non_contiguous_dma(reason="base[128 t + p] goes to partition p, column t"):
             nc.sync.dma_start(base_t[:], base.rearrange("(t p) -> p t", p=P))
-
-        tab2_w = keep.tile([P, 2, T3], I32, name="tab2_w", tag="table_words", align_bytes=64)
+        tab2_word_t = keep.tile([P, 2, T2], I32, name="tab2_word_t", tag="table_words", align_bytes=64)
         for a in range(2):
-            nc.sync.dma_start(tab2_w[:, a, :], tab2_words[a].rearrange("p t i -> p (t i)").bitcast(I32))
+            nc.sync.dma_start(tab2_word_t[:, a, :], tab2_words[a].rearrange("p t i -> p (t i)").bitcast(I32))
 
-        th, hh = {}, {}
+        tanh_y2, summed = {}, {}
 
         def tanh_tile(u):
-            th[u] = keep.tile([P, S], F32, name="th%d" % u, tag="th%d" % u, align_bytes=64)
+            tanh_y2[u] = keep.tile([P, S], F32, name="tanh_y2_%d" % u, tag="row_tile%d" % u, align_bytes=64)
             for half in range(2):
-                y2 = bank([P, BANK], "y2")
-                nc.tensor.matmul_mx(out=y2[:], lhsT=w2_c[:, 256 * u:256 * u + 256].bitcast(FP4X4),
-                                    lhsT_scale=w2_s[:, P * u:P * u + P],
-                                    rhs=v_w[half][:].bitcast(FP8X4), rhs_scale=v_s[half][:], start=True, stop=True)
-                nc.scalar.activation(out=th[u][:, BANK * half:BANK * half + BANK], in_=y2[:], func=ACT.Tanh)
+                y2 = next_bank([P, BANK], "y2")
+                nc.tensor.matmul_mx(out=y2[:], lhsT=w2_codes[:, 2 * P * u:2 * P * (u + 1)].bitcast(FP4X4),
+                                    lhsT_scale=w2_plane[:, P * u:P * (u + 1)],
+                                    rhs=v_codes[half][:].bitcast(FP8X4), rhs_scale=v_plane[half][:], start=True, stop=True)
+                nc.scalar.activation(out=tanh_y2[u][:, BANK * half:BANK * (half + 1)], in_=y2[:], func=ACT.Tanh)
 
-        def join_tile(u):
+        def y1_bank(u, half):
             b, i = divmod(u, PACK)
-            hh[u] = th[u] if u < 7 else keep.tile([P, S], F32, name="hh7", tag="x10_woven", align_bytes=64)
+            y1 = next_bank([P, BANK], "y1")
+            nc.tensor.matmul_mx(out=y1[:], lhsT=w1_codes[b][:, P * i:P * (i + 1)].bitcast(FP8X4),
+                                lhsT_scale=w1_plane[b][:, P * i:P * (i + 1)],
+                                rhs=v_codes[half][:].bitcast(FP8X4), rhs_scale=v_plane[half][:], start=True, stop=True)
+            return y1
+
+        def sum_on_vector(u, dst):
+            summed[u] = dst
             for half in range(2):
-                y1 = bank([P, BANK], "y1")
-                nc.tensor.matmul_mx(out=y1[:], lhsT=w1_c[b][:, P * i:P * i + P].bitcast(FP8X4),
-                                    lhsT_scale=w1_s[b][:, P * i:P * i + P],
-                                    rhs=v_w[half][:].bitcast(FP8X4), rhs_scale=v_s[half][:], start=True, stop=True)
-                cols = slice(BANK * half, BANK * half + BANK)
-                if u in OFF:
-                    paced = keep.tile([P, BANK], F32, name="paced", tag="paced%d%d" % (u, half), align_bytes=64)
-                    nc.scalar.activation(out=paced[:], in_=y1[:], func=ACT.Copy, scale=pace_t[:, b, i:i + 1])
-                    nc.gpsimd.tensor_tensor(hh[u][:, cols], paced[:], th[u][:, cols], ALU.add)
-                else:
-                    nc.vector.scalar_tensor_tensor(out=hh[u][:, cols], in0=y1[:], scalar=pace_t[:, b, i:i + 1],
-                                                   in1=th[u][:, cols], op0=ALU.mult, op1=ALU.add)
+                cols = slice(BANK * half, BANK * (half + 1))
+                nc.vector.scalar_tensor_tensor(out=dst[:, cols], in0=y1_bank(u, half)[:], scalar=pace_t[:, u // PACK, u % PACK:u % PACK + 1],
+                                               in1=tanh_y2[u][:, cols], op0=ALU.mult, op1=ALU.add)
 
-        def pick_one(picked, pos_t, b, i, j0, width):
-            nc.vector.tensor_copy(picked[:, i, :], hh[PACK * b + i][:].indirect(pos_t[:, j0 // 16:(j0 + width) // 16]))
-
-        def pick(picked, pos_t, b, j0, width):
-            for i in range(PACK):
-                pick_one(picked, pos_t, b, i, j0, width)
-
-        def affine_one(planes, picked, with_down, b, i, eng):
-            if eng == "G":
-                nc.gpsimd.tensor_scalar(out=planes[:, i, :], in0=picked[:, i, :], scalar1=gain_t[:, b, i:i + 1],
-                                        scalar2=down_t[:, b, i:i + 1] if with_down else 0.0, op0=ALU.mult, op1=ALU.add)
-            elif with_down:
-                nc.scalar.activation(out=planes[:, i, :], in_=picked[:, i, :], func=ACT.Identity,
-                                     scale=gain_t[:, b, i:i + 1], bias=down_t[:, b, i:i + 1])
-            else:
-                nc.scalar.activation(out=planes[:, i, :], in_=picked[:, i, :], func=ACT.Copy, scale=gain_t[:, b, i:i + 1])
-
-        def affine(picked, with_down, b, width, name, eng, tag):
-            planes = keep.tile([P, PACK, width], BF16, name=name + "_planes", tag=tag, align_bytes=64)
-            for i in range(PACK):
-                affine_one(planes, picked, with_down, b, i, eng)
-            return planes
-
-        def weave(planes, width, name, copy, tag=None):
-            woven = keep.tile([P, width, PACK], BF16, name=name + "_woven", tag=tag or name + "_woven", align_bytes=64)
-            copy(woven[:].rearrange("p (c n) i -> p c i n", n=4), planes[:].rearrange("p i (c n) -> p c i n", n=4))
-            return woven
-
-        def weave_gpsimd(planes, width, name):
-            woven = keep.tile([P, width, PACK], BF16, name=name + "_woven", tag=name + "_woven", align_bytes=64)
-            gpsimd_round(woven[:], planes[:].rearrange("p i n -> p n i"))
-            return woven
-
-        def quantise_x(woven, width, name, tag=None):
-            codes = keep.tile([P, width], U32, name=name + "_c", tag=tag or name + "_c", align_bytes=64)
-            scales = keep.tile([P, width], U8, name=name + "_s", align_bytes=64)
-            nc.vector.quantize_mx(out=codes[:].bitcast(FP8X4), scales=scales[:], in_=woven[:].rearrange("p n i -> p (n i)"))
-            return codes, scales
-
-        picked10 = keep.tile([P, PACK, PJ], F32, name="picked10")
-        picked20 = keep.tile([P, PACK, PJ], F32, name="picked20")
-        picked11 = keep.tile([P, PACK, PJ], F32, name="picked11")
-        v2_s = keep.tile([P, S2], U8, name="v2_s", tag="w1_grouped0", align_bytes=64)
-        nc.vector.tensor_copy(v2_s[:], tab2_s[:].indirect(offs2_t[:]))
-        for u in range(4):
-            tanh_tile(u)
-            join_tile(u)
-            if u == CAST_AT:
+        def sum_on_gpsimd(u):
+            summed[u] = tanh_y2[u]
+            scale = pace_t[:, u // PACK, u % PACK:u % PACK + 1]
+            if u == LAST_SHARED:
                 for half in range(2):
-                    if CAST[half] == "S":
-                        round_w1(1, half, grouped[1], nc.scalar.copy)
-                quantise_w1(1, grouped[1])
-                v2_w.append(keep.tile([P, S2], U32, name="v2_w1", tag="w1_grouped1", align_bytes=64))
-                nc.vector.tensor_copy(v2_w[1][:], tab2_w[:, 1, :].bitcast(U32).indirect(offs2_t[:]))
-            pick_one(picked10, pos1_t, 0, u, 0, PJ)
-            pick_one(picked20, pos2_t, 0, u, 0, PJ)
-            if u == 1:
-                v2_w = [keep.tile([P, S2], U32, name="v2_w0", align_bytes=64)]
-                nc.vector.tensor_copy(v2_w[0][:], tab2_w[:, 0, :].bitcast(U32).indirect(offs2_t[:]))
-        for u in range(4, 8):
+                    cols = slice(BANK * half, BANK * (half + 1))
+                    y1 = y1_bank(u, half)
+                    paced = keep.tile([P, BANK], F32, name="paced", tag="paced%d_%d" % (u, half), align_bytes=64)
+                    nc.scalar.activation(out=paced[:], in_=y1[:], func=ACT.Copy, scale=scale)
+                    nc.gpsimd.tensor_tensor(summed[u][:, cols], paced[:], tanh_y2[u][:, cols], ALU.add)
+            else:
+                paced = keep.tile([P, S], F32, name="paced", tag="paced%d" % u, align_bytes=64)
+                for half in range(2):
+                    nc.scalar.activation(out=paced[:, BANK * half:BANK * (half + 1)], in_=y1_bank(u, half)[:], func=ACT.Copy, scale=scale)
+                nc.gpsimd.tensor_tensor(summed[u][:], paced[:], tanh_y2[u][:], ALU.add)
+
+        def pick(picked, pos_t, u, j0, width):
+            nc.vector.tensor_copy(picked[:, u % PACK, :], summed[u][:].indirect(pos_t[:, j0 // PER_COLUMN:(j0 + width) // PER_COLUMN]))
+
+        def finish_x1(rows, picked, b):
+            for i in range(PACK):
+                nc.scalar.activation(out=rows[:, i, :], in_=picked[:, i, :], func=ACT.Copy, scale=gain_t[:, b, i:i + 1])
+
+        def finish_x2(rows, picked, b, tensor_scalar):
+            for i in range(PACK):
+                tensor_scalar(out=rows[:, i, :], in0=picked[:, i, :], scalar1=gain_t[:, b, i:i + 1],
+                              scalar2=down_t[:, b, i:i + 1], op0=ALU.mult, op1=ALU.add)
+
+        def finish_x2_on_scalar(rows, picked, b):
+            for i in range(PACK):
+                nc.scalar.activation(out=rows[:, i, :], in_=picked[:, i, :], func=ACT.Identity,
+                                     scale=gain_t[:, b, i:i + 1], bias=down_t[:, b, i:i + 1])
+
+        def interleave(rows, width, name, tag, copy):
+            woven = keep.tile([P, width, PACK], BF16, name=name, tag=tag, align_bytes=64)
+            copy(woven[:].rearrange("p (c n) i -> p c i n", n=4), rows[:].rearrange("p i (c n) -> p c i n", n=4))
+            return woven
+
+        def quantise_x(woven, width, name, tag):
+            codes = keep.tile([P, width], U32, name=name + "_codes", tag=tag, align_bytes=64)
+            plane = keep.tile([P, width], U8, name=name + "_plane", align_bytes=64)
+            nc.vector.quantize_mx(out=codes[:].bitcast(FP8X4), scales=plane[:], in_=woven[:].rearrange("p n i -> p (n i)"))
+            return codes, plane
+
+        def gather_v2_codes(a, tag):
+            codes = keep.tile([P, HUTS], U32, name="v2_codes%d" % a, tag=tag, align_bytes=64)
+            nc.vector.tensor_copy(codes[:], tab2_word_t[:, a, :].bitcast(U32).indirect(offs2_t[:]))
+            return codes
+
+        x1a_picked = keep.tile([P, PACK, PAIRS], F32, name="x1a_picked")
+        x2a_picked = keep.tile([P, PACK, PAIRS], F32, name="x2a_picked")
+        x1b_picked = keep.tile([P, PACK, PAIRS], F32, name="x1b_picked")
+        v2_plane = keep.tile([P, HUTS], U8, name="v2_plane", tag="w1_bf16_0", align_bytes=64)
+        nc.vector.tensor_copy(v2_plane[:], tab2_scale_t[:].indirect(offs2_t[:]))
+        v2_codes = {}
+        for u in range(PACK):
             tanh_tile(u)
-            if u in OFF:
-                join_tile(u)
-        last = max(OFF)
-        planes10 = keep.tile([P, PACK, PJ], BF16, name="x10_planes", tag="paced%d0" % last, align_bytes=64)
-        planes20 = keep.tile([P, PACK, PJ], BF16, name="x20_planes", tag="paced%d1" % last, align_bytes=64)
-        for i in range(PACK):
-            affine_one(planes10, picked10, False, 0, i, AFF[0])
-        for i in range(PACK):
-            affine_one(planes20, picked20, True, 0, i, AFF[1])
-        woven10 = weave(planes10, PJ, "x10", nc.scalar.copy)
-        woven20 = weave(planes20, PJ, "x20", nc.scalar.copy, "paced%d0" % last)
-        for u in range(4, 8):
-            if u == 7:
-                x10 = quantise_x(woven10, PJ, "x10")
-            if u not in OFF:
-                join_tile(u)
-            pick_one(picked11, pos1_t, 1, u - 4, 0, PJ)
-        planes11 = keep.tile([P, PACK, PJ], BF16, name="x11_planes", tag="paced%d1" % last, align_bytes=64)
-        for i in range(PACK):
-            affine_one(planes11, picked11, False, 1, i, AFF[2])
-        woven11 = weave(planes11, PJ, "x11", nc.scalar.copy)
+            if u < FIRST_SHARED:
+                sum_on_vector(u, tanh_y2[u])
+            else:
+                sum_on_gpsimd(u)
+            if u == W1_SECOND_AFTER:
+                round_w1(1, 1, nc.scalar.copy)
+                quantise_w1(1, ((0, PACK),))
+                v2_codes[1] = gather_v2_codes(1, "w1_bf16_1")
+            pick(x1a_picked, pos1_t, u, 0, PAIRS)
+            pick(x2a_picked, pos2_t, u, 0, PAIRS)
+            if u == FIRST_SHARED:
+                v2_codes[0] = gather_v2_codes(0, "v2_codes0")
 
-        planes21, woven21 = [], []
+        for u in range(PACK, ROW_TILES):
+            tanh_tile(u)
+            if u <= LAST_SHARED:
+                sum_on_gpsimd(u)
+        first_chain, second_chain = "paced%d_0" % LAST_SHARED, "paced%d_1" % LAST_SHARED
+        x1a_rows = keep.tile([P, PACK, PAIRS], BF16, name="x1a_rows", tag=first_chain, align_bytes=64)
+        x2a_rows = keep.tile([P, PACK, PAIRS], BF16, name="x2a_rows", tag=second_chain, align_bytes=64)
+        finish_x1(x1a_rows, x1a_picked, 0)
+        finish_x2(x2a_rows, x2a_picked, 0, nc.gpsimd.tensor_scalar)
+        x1a_woven = interleave(x1a_rows, PAIRS, "x1a_woven", "x1a_woven", nc.scalar.copy)
+        x2a_woven = interleave(x2a_rows, PAIRS, "x2a_woven", first_chain, nc.scalar.copy)
+        for u in range(PACK, ROW_TILES - 1):
+            if u > LAST_SHARED:
+                sum_on_vector(u, tanh_y2[u])
+            pick(x1b_picked, pos1_t, u, 0, PAIRS)
+        last = ROW_TILES - 1
+        x1a = quantise_x(x1a_woven, PAIRS, "x1a", "x1a_codes")
+        summed_last = keep.tile([P, S], F32, name="summed_last", tag="x1a_woven", align_bytes=64)
+        sum_on_vector(last, summed_last)
+        pick(x1b_picked, pos1_t, last, 0, PAIRS)
+        x1b_rows = keep.tile([P, PACK, PAIRS], BF16, name="x1b_rows", tag=second_chain, align_bytes=64)
+        finish_x1(x1b_rows, x1b_picked, 1)
+        x1b_woven = interleave(x1b_rows, PAIRS, "x1b_woven", "x1b_woven", nc.scalar.copy)
 
-        def pick21(c, tag):
-            j0, width = CHUNKS[c]
-            picked = keep.tile([P, PACK, width], F32, name="picked21%d" % c, tag=tag, align_bytes=64)
-            pick(picked, pos2_t, 1, j0, width)
-            planes21.append(affine(picked, True, 1, width, "x21%d" % c, AFF[3 + c], "planes21%d" % c))
+        x2a = quantise_x(x2a_woven, PAIRS, "x2a", "row_tile%d" % last)
+        chunk0_picked = keep.tile([P, PACK, CHUNK], F32, name="chunk0_picked", tag=first_chain, align_bytes=64)
+        for u in range(PACK, ROW_TILES):
+            pick(chunk0_picked, pos2_t, u, 0, CHUNK)
+        chunk0_rows = keep.tile([P, PACK, CHUNK], BF16, name="chunk0_rows", align_bytes=64)
+        finish_x2(chunk0_rows, chunk0_picked, 1, nc.vector.tensor_scalar)
+        x1b = quantise_x(x1b_woven, PAIRS, "x1b", "x1b_codes")
 
-        x20 = quantise_x(woven20, PJ, "x20", "th7")
-        pick21(0, "paced%d0" % last)
-        x11 = quantise_x(woven11, PJ, "x11")
+        def score(dst, a, t, codes, plane, start, stop):
+            nc.tensor.matmul_mx(out=dst, lhsT=v2_codes[a][:, P * t:P * (t + 1)].bitcast(FP8X4),
+                                lhsT_scale=v2_plane[PACK * a:P, P * t:P * (t + 1)],
+                                rhs=codes.bitcast(FP8X4), rhs_scale=plane, start=start, stop=stop)
 
-        def score(dst, a, mt, codes, scales, start, stop):
-            nc.tensor.matmul_mx(out=dst, lhsT=v2_w[a][:, P * mt:P * mt + P].bitcast(FP8X4),
-                                lhsT_scale=v2_s[4 * a:P, P * mt:P * mt + P],
-                                rhs=codes.bitcast(FP8X4), rhs_scale=scales, start=start, stop=stop)
+        e1_sb = keep.tile([P, HUT_TILES, PAIRS], F32, name="e1_sb")
+        e1 = [next_bank([P, PAIRS], "e1") for t in range(HUT_TILES)]
+        for t in range(HUT_TILES):
+            score(e1[t][:], 0, t, x1a[0][:], x1a[1][:], True, False)
+        for t in range(HUT_TILES):
+            score(e1[t][:], 1, t, x1b[0][:], x1b[1][:], False, True)
+        per_bank = BANK // CHUNK
+        e2 = {}
+        for c in range(2):
+            cols = slice(CHUNK * c, CHUNK * (c + 1))
+            for t0 in range(0, HUT_TILES, per_bank):
+                e2[c, t0] = next_bank([P, per_bank, CHUNK], "e2")
+                for s in range(per_bank):
+                    score(e2[c, t0][:, s, :], 0, t0 + s, x2a[0][:, cols], x2a[1][:, cols], s == 0, False)
 
-        e1_s = keep.tile([P, 4, PJ], F32, name="e1_s")
-        e1 = [bank([P, PJ], "e1") for mt in range(4)]
-        for mt in range(4):
-            score(e1[mt][:], 0, mt, x10[0][:], x10[1][:], True, False)
-        for mt in range(4):
-            score(e1[mt][:], 1, mt, x11[0][:], x11[1][:], False, True)
-        e2 = []
-        for c, (j0, width) in enumerate(CHUNKS):
-            per = BANK // width
-            for mt0 in range(0, 4, per):
-                acc = bank([P, per, width], "e2")
-                e2.append((c, mt0, per, acc))
-                for s in range(per):
-                    score(acc[:, s, :], 0, mt0 + s, x20[0][:, j0:j0 + width], x20[1][:, j0:j0 + width], s == 0, False)
+        chunk_woven = [interleave(chunk0_rows, CHUNK, "chunk0_woven", second_chain, nc.scalar.copy)]
+        for t in range(E1_EARLY):
+            nc.scalar.copy(e1_sb[:, t, :], e1[t][:])
+        chunk1_picked = keep.tile([P, PACK, CHUNK], F32, name="chunk1_picked", tag="x1b_woven", align_bytes=64)
+        for u in range(PACK, ROW_TILES):
+            pick(chunk1_picked, pos2_t, u, CHUNK, CHUNK)
+        chunk1_rows = keep.tile([P, PACK, CHUNK], BF16, name="chunk1_rows", align_bytes=64)
+        finish_x2_on_scalar(chunk1_rows, chunk1_picked, 1)
+        for t in range(E1_EARLY, HUT_TILES):
+            nc.scalar.copy(e1_sb[:, t, :], e1[t][:])
+        chunk_woven.append(interleave(chunk1_rows, CHUNK, "chunk1_woven", "chunk1_woven", nc.vector.tensor_copy))
+        for c in range(2):
+            codes, plane = quantise_x(chunk_woven[c], CHUNK, "chunk%d" % c, "chunk%d_codes" % c)
+            for t0 in range(0, HUT_TILES, per_bank):
+                for s in range(per_bank):
+                    score(e2[c, t0][:, s, :], 1, t0 + s, codes[:], plane[:], False, s == per_bank - 1)
 
-        woven21.append(weave(planes21[0], CHUNKS[0][1], "x210", nc.scalar.copy))
-        pick21(1, "x11_woven")
-        if len(CHUNKS) > 2:
-            pick21(2, "planes210")
-        for mt in range(4):
-            nc.scalar.copy(e1_s[:, mt, :], e1[mt][:])
-        for c in range(1, len(CHUNKS)):
-            woven21.append(weave(planes21[c], CHUNKS[c][1], "x21%d" % c, nc.vector.tensor_copy))
-        out_v = out.rearrange("(t p) j -> p t j", p=P)
-        for c, (j0, width) in enumerate(CHUNKS):
-            name = "x21%d" % c
-            codes, scales = quantise_x(woven21[c], width, name)
-            for cc, mt0, per, acc in e2:
-                if cc == c:
-                    for s in range(per):
-                        score(acc[:, s, :], 1, mt0 + s, codes[:], scales[:], False, s == per - 1)
-        for c, bank_mt0, per, acc in e2:
-            j0, width = CHUNKS[c]
-            step = 2 if c >= SPLIT else per
-            for s0 in range(0, per, step):
-                mt0 = bank_mt0 + s0
-                res = keep.tile([P, step, width], F32, name="res%d%d" % (c, mt0), align_bytes=64,
-                                tag="x21%d_woven" % (len(CHUNKS) - 1) if (c, mt0) == (0, 0) else "res%d%d" % (c, mt0))
-                nc.vector.tensor_tensor(res[:], acc[:, s0:s0 + step, :], e1_s[:, mt0:mt0 + step, j0:j0 + width], ALU.mult)
-                for s in range(step):
-                    mt = mt0 + s
-                    nc.scalar.activation(out=res[:, s, :], in_=res[:, s, :], func=ACT.Identity, bias=base_t[:, mt:mt + 1])
-                nc.sync.dma_start(out_v[:, mt0:mt0 + step, j0:j0 + width], res[:])
+        out_by_tile = out.rearrange("(t p) j -> p t j", p=P)
+        for c in range(2):
+            cols = slice(CHUNK * c, CHUNK * (c + 1))
+            for t0 in range(0, HUT_TILES, per_bank):
+                result = keep.tile([P, per_bank, CHUNK], F32, name="result%d%d" % (c, t0), align_bytes=64,
+                                   tag="chunk1_woven" if (c, t0) == (0, 0) else "result%d%d" % (c, t0))
+                nc.vector.tensor_tensor(result[:], e2[c, t0][:], e1_sb[:, t0:t0 + per_bank, cols], ALU.mult)
+                for s in range(per_bank):
+                    nc.scalar.activation(out=result[:, s, :], in_=result[:, s, :], func=ACT.Identity,
+                                         bias=base_t[:, t0 + s:t0 + s + 1])
+                nc.sync.dma_start(out_by_tile[:, t0:t0 + per_bank, cols], result[:])

from contextlib import ExitStack

import concourse.mybir as mybir

K, H, T, S, PAIRS, T2, HUTS = 512, 1024, 4096, 1024, 512, 2048, 512
FLOPS = 2 * (2 * K * H * S + 2 * H * HUTS * PAIRS)

F32 = mybir.dt.float32
BF16 = mybir.dt.bfloat16
I32 = mybir.dt.int32
U32 = mybir.dt.uint32
U16 = mybir.dt.uint16
U8 = mybir.dt.uint8
FP8X4 = mybir.dt.float8_e4m3fn_x4
FP4X4 = mybir.dt.float4_e2m1fn_x4
ACT = mybir.ActivationFunctionType
ALU = mybir.AluOpType

P = 128
PACK = 4
PER_COLUMN = 16
BANK = 512
BANKS = 8
ROW_TILES = H // P
HUT_TILES = HUTS // P
W1_PIECE = 256
CHUNK = PAIRS // 2
FIRST_SHARED, LAST_SHARED = 1, 5
W1_SECOND_AFTER = 2
E1_EARLY = 2


def tile_list_next_hut_advice_kernel(tc, tab_words, tab_scales, offs, tab2_words, tab2_scales, offs2, pos1, pos2,
                                               w1, w2_words, w2_scales, pace, gain, down, base, out):
    nc = tc.nc
    with ExitStack() as ctx:
        lists = ctx.enter_context(tc.tile_pool(name="lists", bufs=1))
        keep = ctx.enter_context(tc.tile_pool(name="keep", bufs=1))
        psum = ctx.enter_context(tc.psum_pool(name="psum", bufs=1))

        banks_taken = []

        def next_bank(shape, name):
            banks_taken.append(name)
            return psum.tile(shape, F32, name=name, tag="bank%d" % (len(banks_taken) % BANKS))

        offs_t = lists.tile([P, S // PER_COLUMN], U16, name="offs_t")
        offs2_t = lists.tile([P, HUTS // PER_COLUMN], U16, name="offs2_t")
        pos1_t = lists.tile([P, PAIRS // PER_COLUMN], U16, name="pos1_t")
        pos2_t = lists.tile([P, PAIRS // PER_COLUMN], U16, name="pos2_t")

        w2_scales_raw = keep.tile([P, H], U8, name="w2_scales_raw", tag="w2_scales_raw", align_bytes=64)
        nc.vector.memset(w2_scales_raw[:].bitcast(I32), 0)
        tab_scale_t = keep.tile([P, T], U8, name="tab_scale_t", tag="tab_scale_t", align_bytes=64)
        nc.vector.memset(tab_scale_t[:].bitcast(I32), 0)
        tab2_scale_t = keep.tile([P, T2], U8, name="tab2_scale_t", align_bytes=64)
        nc.vector.memset(tab2_scale_t[:].bitcast(I32), 0)

        def load_w1(b, piece, tag):
            raw = keep.tile([P, PACK, W1_PIECE], F32, name="w1_raw%d%d" % (b, piece), tag=tag, align_bytes=64)
            c0 = BANK * b + W1_PIECE * piece
            nc.sync.dma_start(raw[:], w1.rearrange("(p j) c -> p j c", j=PACK)[:, :, c0:c0 + W1_PIECE])
            return raw

        def load_by_row(vec, name):
            vec_t = keep.tile([P, 2, PACK], F32, name=name)
            nc.sync.dma_start(vec_t[:], vec.rearrange("(b p i) -> p b i", b=2, i=PACK))
            return vec_t

        nc.sync.dma_start(offs_t[:], offs)
        nc.sync.dma_start(offs2_t[:], offs2)
        nc.sync.dma_start(pos1_t[:], pos1)
        nc.sync.dma_start(pos2_t[:], pos2)
        for q in range(4):
            nc.sync.dma_start(w2_scales_raw[32 * q:32 * q + 4, :].bitcast(I32), w2_scales[0, 4 * q:4 * q + 4, :].bitcast(I32))
        for q in range(4):
            nc.sync.dma_start(tab_scale_t[32 * q:32 * q + 4, :].bitcast(I32), tab_scales[0, 4 * q:4 * q + 4, :].bitcast(I32))
        w2_words_raw = keep.tile([P, 2 * H], U8, name="w2_words_raw", align_bytes=64)
        nc.sync.dma_start(w2_words_raw[:].bitcast(I32), w2_words[0].bitcast(I32))
        tab_word_t = keep.tile([P, T], I32, name="tab_word_t", tag="table_words", align_bytes=64)
        nc.sync.dma_start(tab_word_t[:], tab_words[0].rearrange("p t i -> p (t i)").bitcast(I32))
        w1_raw = {(0, 0): load_w1(0, 0, "row_tile0"), (0, 1): load_w1(0, 1, "w1_raw01")}
        pace_t = load_by_row(pace, "pace_t")
        w1_raw[1, 0] = load_w1(1, 0, "w2_scales_raw")
        for q in range(4):
            nc.sync.dma_start(tab2_scale_t[32 * q:32 * q + 8, :].bitcast(I32), tab2_scales[:, 4 * q:4 * q + 4, :].bitcast(I32))
        gain_t = load_by_row(gain, "gain_t")

        w2_codes = keep.tile([P, 2 * H], U8, name="w2_codes", align_bytes=64)
        w2_plane = keep.tile([P, H], U8, name="w2_plane", align_bytes=64)
        nc.vector.tensor_copy(w2_plane[:].rearrange("p (b i m) -> p b i m", b=2, i=PACK),
                              w2_scales_raw[:].rearrange("p (b m i) -> p b i m", b=2, i=PACK))

        half_columns = BANK // PER_COLUMN
        v_plane, v_codes = [], []
        for half in range(2):
            plane = keep.tile([P, BANK], U8, name="v_plane%d" % half, align_bytes=64)
            nc.vector.tensor_copy(plane[:], tab_scale_t[:].indirect(offs_t[:, half_columns * half:half_columns * (half + 1)]))
            v_plane.append(plane)
        nc.vector.tensor_copy(w2_codes[:].bitcast(U16).rearrange("p (b i m) -> p b i m", b=2, i=PACK),
                              w2_words_raw[:].bitcast(U16).rearrange("p (b m i) -> p b i m", b=2, i=PACK))
        for half in range(2):
            codes = keep.tile([P, BANK], U32, name="v_codes%d" % half, align_bytes=64)
            nc.vector.tensor_copy(codes[:], tab_word_t[:].bitcast(U32).indirect(offs_t[:, half_columns * half:half_columns * (half + 1)]))
            v_codes.append(codes)

        w1_codes, w1_plane = {}, {}
        w1_bf16 = [keep.tile([P, PACK, P, PACK], BF16, name="w1_bf16_%d" % b, tag="w1_bf16_%d" % b, align_bytes=64) for b in range(2)]

        def round_w1(b, piece, copy):
            m0, m1 = W1_PIECE // PACK * piece, W1_PIECE // PACK * (piece + 1)
            copy(w1_bf16[b][:, :, m0:m1, :].rearrange("p i m j -> p m i j"),
                 w1_raw[b, piece][:].rearrange("p j (m i) -> p m i j", i=PACK))

        def gpsimd_round(dst, src):
            nc.gpsimd.tensor_scalar(out=dst, in0=src, scalar1=1.0, scalar2=0.0, op0=ALU.mult, op1=ALU.add)

        def quantise_w1(b, cuts):
            w1_codes[b] = keep.tile([P, BANK], U32, name="w1_codes%d" % b, align_bytes=64)
            w1_plane[b] = keep.tile([P, BANK], U8, name="w1_plane%d" % b, align_bytes=64)
            for i0, i1 in cuts:
                nc.vector.quantize_mx(out=w1_codes[b][:, P * i0:P * i1].bitcast(FP8X4), scales=w1_plane[b][:, P * i0:P * i1],
                                      in_=w1_bf16[b][:, i0:i1].rearrange("p i m j -> p (i m j)"))

        round_w1(0, 0, nc.scalar.copy)
        round_w1(0, 1, nc.vector.tensor_copy)
        quantise_w1(0, ((0, 1), (1, PACK)))
        round_w1(1, 0, gpsimd_round)
        w1_raw[1, 1] = load_w1(1, 1, "tab_scale_t")
        down_t = load_by_row(down, "down_t")
        base_t = keep.tile([P, HUT_TILES], F32, name="base_t")
        with nc.allow_non_contiguous_dma(reason="base[128 t + p] goes to partition p, column t"):
            nc.sync.dma_start(base_t[:], base.rearrange("(t p) -> p t", p=P))
        tab2_word_t = keep.tile([P, 2, T2], I32, name="tab2_word_t", tag="table_words", align_bytes=64)
        for a in range(2):
            nc.sync.dma_start(tab2_word_t[:, a, :], tab2_words[a].rearrange("p t i -> p (t i)").bitcast(I32))

        tanh_y2, summed = {}, {}

        def tanh_tile(u):
            tanh_y2[u] = keep.tile([P, S], F32, name="tanh_y2_%d" % u, tag="row_tile%d" % u, align_bytes=64)
            for half in range(2):
                y2 = next_bank([P, BANK], "y2")
                nc.tensor.matmul_mx(out=y2[:], lhsT=w2_codes[:, 2 * P * u:2 * P * (u + 1)].bitcast(FP4X4),
                                    lhsT_scale=w2_plane[:, P * u:P * (u + 1)],
                                    rhs=v_codes[half][:].bitcast(FP8X4), rhs_scale=v_plane[half][:], start=True, stop=True)
                nc.scalar.activation(out=tanh_y2[u][:, BANK * half:BANK * (half + 1)], in_=y2[:], func=ACT.Tanh)

        def y1_bank(u, half):
            b, i = divmod(u, PACK)
            y1 = next_bank([P, BANK], "y1")
            nc.tensor.matmul_mx(out=y1[:], lhsT=w1_codes[b][:, P * i:P * (i + 1)].bitcast(FP8X4),
                                lhsT_scale=w1_plane[b][:, P * i:P * (i + 1)],
                                rhs=v_codes[half][:].bitcast(FP8X4), rhs_scale=v_plane[half][:], start=True, stop=True)
            return y1

        def sum_on_vector(u, dst):
            summed[u] = dst
            for half in range(2):
                cols = slice(BANK * half, BANK * (half + 1))
                nc.vector.scalar_tensor_tensor(out=dst[:, cols], in0=y1_bank(u, half)[:], scalar=pace_t[:, u // PACK, u % PACK:u % PACK + 1],
                                               in1=tanh_y2[u][:, cols], op0=ALU.mult, op1=ALU.add)

        def sum_on_gpsimd(u):
            summed[u] = tanh_y2[u]
            scale = pace_t[:, u // PACK, u % PACK:u % PACK + 1]
            if u == LAST_SHARED:
                for half in range(2):
                    cols = slice(BANK * half, BANK * (half + 1))
                    y1 = y1_bank(u, half)
                    paced = keep.tile([P, BANK], F32, name="paced", tag="paced%d_%d" % (u, half), align_bytes=64)
                    nc.scalar.activation(out=paced[:], in_=y1[:], func=ACT.Copy, scale=scale)
                    nc.gpsimd.tensor_tensor(summed[u][:, cols], paced[:], tanh_y2[u][:, cols], ALU.add)
            else:
                paced = keep.tile([P, S], F32, name="paced", tag="paced%d" % u, align_bytes=64)
                for half in range(2):
                    nc.scalar.activation(out=paced[:, BANK * half:BANK * (half + 1)], in_=y1_bank(u, half)[:], func=ACT.Copy, scale=scale)
                nc.gpsimd.tensor_tensor(summed[u][:], paced[:], tanh_y2[u][:], ALU.add)

        def pick(picked, pos_t, u, j0, width):
            nc.vector.tensor_copy(picked[:, u % PACK, :], summed[u][:].indirect(pos_t[:, j0 // PER_COLUMN:(j0 + width) // PER_COLUMN]))

        def finish_x1(rows, picked, b):
            for i in range(PACK):
                nc.scalar.activation(out=rows[:, i, :], in_=picked[:, i, :], func=ACT.Copy, scale=gain_t[:, b, i:i + 1])

        def finish_x2(rows, picked, b, tensor_scalar):
            for i in range(PACK):
                tensor_scalar(out=rows[:, i, :], in0=picked[:, i, :], scalar1=gain_t[:, b, i:i + 1],
                              scalar2=down_t[:, b, i:i + 1], op0=ALU.mult, op1=ALU.add)

        def finish_x2_on_scalar(rows, picked, b):
            for i in range(PACK):
                nc.scalar.activation(out=rows[:, i, :], in_=picked[:, i, :], func=ACT.Identity,
                                     scale=gain_t[:, b, i:i + 1], bias=down_t[:, b, i:i + 1])

        def interleave(rows, width, name, tag, copy):
            woven = keep.tile([P, width, PACK], BF16, name=name, tag=tag, align_bytes=64)
            copy(woven[:].rearrange("p (c n) i -> p c i n", n=4), rows[:].rearrange("p i (c n) -> p c i n", n=4))
            return woven

        def quantise_x(woven, width, name, tag):
            codes = keep.tile([P, width], U32, name=name + "_codes", tag=tag, align_bytes=64)
            plane = keep.tile([P, width], U8, name=name + "_plane", align_bytes=64)
            nc.vector.quantize_mx(out=codes[:].bitcast(FP8X4), scales=plane[:], in_=woven[:].rearrange("p n i -> p (n i)"))
            return codes, plane

        def gather_v2_codes(a, tag):
            codes = keep.tile([P, HUTS], U32, name="v2_codes%d" % a, tag=tag, align_bytes=64)
            nc.vector.tensor_copy(codes[:], tab2_word_t[:, a, :].bitcast(U32).indirect(offs2_t[:]))
            return codes

        x1a_picked = keep.tile([P, PACK, PAIRS], F32, name="x1a_picked")
        x2a_picked = keep.tile([P, PACK, PAIRS], F32, name="x2a_picked")
        x1b_picked = keep.tile([P, PACK, PAIRS], F32, name="x1b_picked")
        v2_plane = keep.tile([P, HUTS], U8, name="v2_plane", tag="w1_bf16_0", align_bytes=64)
        nc.vector.tensor_copy(v2_plane[:], tab2_scale_t[:].indirect(offs2_t[:]))
        v2_codes = {}
        for u in range(PACK):
            tanh_tile(u)
            if u < FIRST_SHARED:
                sum_on_vector(u, tanh_y2[u])
            else:
                sum_on_gpsimd(u)
            if u == W1_SECOND_AFTER:
                round_w1(1, 1, nc.scalar.copy)
                quantise_w1(1, ((0, PACK),))
                v2_codes[1] = gather_v2_codes(1, "w1_bf16_1")
            pick(x1a_picked, pos1_t, u, 0, PAIRS)
            pick(x2a_picked, pos2_t, u, 0, PAIRS)
            if u == FIRST_SHARED:
                v2_codes[0] = gather_v2_codes(0, "v2_codes0")

        for u in range(PACK, ROW_TILES):
            tanh_tile(u)
            if u <= LAST_SHARED:
                sum_on_gpsimd(u)
        first_chain, second_chain = "paced%d_0" % LAST_SHARED, "paced%d_1" % LAST_SHARED
        x1a_rows = keep.tile([P, PACK, PAIRS], BF16, name="x1a_rows", tag=first_chain, align_bytes=64)
        x2a_rows = keep.tile([P, PACK, PAIRS], BF16, name="x2a_rows", tag=second_chain, align_bytes=64)
        finish_x1(x1a_rows, x1a_picked, 0)
        finish_x2(x2a_rows, x2a_picked, 0, nc.gpsimd.tensor_scalar)
        x1a_woven = interleave(x1a_rows, PAIRS, "x1a_woven", "x1a_woven", nc.scalar.copy)
        x2a_woven = interleave(x2a_rows, PAIRS, "x2a_woven", first_chain, nc.scalar.copy)
        for u in range(PACK, ROW_TILES - 1):
            if u > LAST_SHARED:
                sum_on_vector(u, tanh_y2[u])
            pick(x1b_picked, pos1_t, u, 0, PAIRS)
        last = ROW_TILES - 1
        x1a = quantise_x(x1a_woven, PAIRS, "x1a", "x1a_codes")
        summed_last = keep.tile([P, S], F32, name="summed_last", tag="x1a_woven", align_bytes=64)
        sum_on_vector(last, summed_last)
        pick(x1b_picked, pos1_t, last, 0, PAIRS)
        x1b_rows = keep.tile([P, PACK, PAIRS], BF16, name="x1b_rows", tag=second_chain, align_bytes=64)
        finish_x1(x1b_rows, x1b_picked, 1)
        x1b_woven = interleave(x1b_rows, PAIRS, "x1b_woven", "x1b_woven", nc.scalar.copy)

        x2a = quantise_x(x2a_woven, PAIRS, "x2a", "row_tile%d" % last)
        chunk0_picked = keep.tile([P, PACK, CHUNK], F32, name="chunk0_picked", tag=first_chain, align_bytes=64)
        for u in range(PACK, ROW_TILES):
            pick(chunk0_picked, pos2_t, u, 0, CHUNK)
        chunk0_rows = keep.tile([P, PACK, CHUNK], BF16, name="chunk0_rows", align_bytes=64)
        finish_x2(chunk0_rows, chunk0_picked, 1, nc.vector.tensor_scalar)
        x1b = quantise_x(x1b_woven, PAIRS, "x1b", "x1b_codes")

        def score(dst, a, t, codes, plane, start, stop):
            nc.tensor.matmul_mx(out=dst, lhsT=v2_codes[a][:, P * t:P * (t + 1)].bitcast(FP8X4),
                                lhsT_scale=v2_plane[PACK * a:P, P * t:P * (t + 1)],
                                rhs=codes.bitcast(FP8X4), rhs_scale=plane, start=start, stop=stop)

        e1_sb = keep.tile([P, HUT_TILES, PAIRS], F32, name="e1_sb")
        e1 = [next_bank([P, PAIRS], "e1") for t in range(HUT_TILES)]
        for t in range(HUT_TILES):
            score(e1[t][:], 0, t, x1a[0][:], x1a[1][:], True, False)
        for t in range(HUT_TILES):
            score(e1[t][:], 1, t, x1b[0][:], x1b[1][:], False, True)
        per_bank = BANK // CHUNK
        e2 = {}
        for c in range(2):
            cols = slice(CHUNK * c, CHUNK * (c + 1))
            for t0 in range(0, HUT_TILES, per_bank):
                e2[c, t0] = next_bank([P, per_bank, CHUNK], "e2")
                for s in range(per_bank):
                    score(e2[c, t0][:, s, :], 0, t0 + s, x2a[0][:, cols], x2a[1][:, cols], s == 0, False)

        chunk_woven = [interleave(chunk0_rows, CHUNK, "chunk0_woven", second_chain, nc.scalar.copy)]
        for t in range(E1_EARLY):
            nc.scalar.copy(e1_sb[:, t, :], e1[t][:])
        chunk1_picked = keep.tile([P, PACK, CHUNK], F32, name="chunk1_picked", tag="x1b_woven", align_bytes=64)
        for u in range(PACK, ROW_TILES):
            pick(chunk1_picked, pos2_t, u, CHUNK, CHUNK)
        chunk1_rows = keep.tile([P, PACK, CHUNK], BF16, name="chunk1_rows", align_bytes=64)
        finish_x2_on_scalar(chunk1_rows, chunk1_picked, 1)
        for t in range(E1_EARLY, HUT_TILES):
            nc.scalar.copy(e1_sb[:, t, :], e1[t][:])
        chunk_woven.append(interleave(chunk1_rows, CHUNK, "chunk1_woven", "chunk1_woven", nc.vector.tensor_copy))
        for c in range(2):
            codes, plane = quantise_x(chunk_woven[c], CHUNK, "chunk%d" % c, "chunk%d_codes" % c)
            for t0 in range(0, HUT_TILES, per_bank):
                for s in range(per_bank):
                    score(e2[c, t0][:, s, :], 1, t0 + s, codes[:], plane[:], False, s == per_bank - 1)

        out_by_tile = out.rearrange("(t p) j -> p t j", p=P)
        for c in range(2):
            cols = slice(CHUNK * c, CHUNK * (c + 1))
            for t0 in range(0, HUT_TILES, per_bank):
                result = keep.tile([P, per_bank, CHUNK], F32, name="result%d%d" % (c, t0), align_bytes=64,
                                   tag="chunk1_woven" if (c, t0) == (0, 0) else "result%d%d" % (c, t0))
                nc.vector.tensor_tensor(result[:], e2[c, t0][:], e1_sb[:, t0:t0 + per_bank, cols], ALU.mult)
                for s in range(per_bank):
                    nc.scalar.activation(out=result[:, s, :], in_=result[:, s, :], func=ACT.Identity,
                                         bias=base_t[:, t0 + s:t0 + s + 1])
                nc.sync.dma_start(out_by_tile[:, t0:t0 + per_bank, cols], result[:])
